import numpy as np
import ml_dtypes


def mxq(x, axis, fmt="e4m3"):
    dtype, down = {"e4m3": (ml_dtypes.float8_e4m3fn, 7), "e5m2": (ml_dtypes.float8_e5m2, 14)}[fmt]
    v = np.moveaxis(np.asarray(x, np.float32).astype(ml_dtypes.bfloat16).astype(np.float64), axis, -1)
    blocks = v.reshape(v.shape[:-1] + (-1, 32))
    amax = np.abs(blocks).max(-1, keepdims=True)
    byte = np.maximum(np.where(amax > 0, np.frexp(amax)[1] - 1 + 127, 0) - down, 1)
    scale = np.exp2(byte - 127.0)
    codes = (blocks / scale).astype(np.float32).astype(dtype).astype(np.float64)
    return np.moveaxis((codes * scale).reshape(v.shape), -1, axis)


WIDE = False


def mx_kscale(k):
    if not WIDE:
        return np.ones(k)
    levels = np.array([10, -10, 5, -5, 0])
    if k % 512:
        return np.exp2(np.random.permutation(np.resize(levels, k // 32))).repeat(32)
    a = np.empty((k // 512, 16))
    for p in range(k // 512):
        a[p, :8] = np.random.permutation(np.resize(levels, 8))
        for g in range(8):
            far = levels[np.abs(levels - a[p, g]) >= 10]
            a[p, g + 8] = far[np.random.randint(len(far))]
    return np.exp2(a.ravel()).repeat(32)


def f64(x):
    return np.asarray(x).astype(np.float64)


def striped(idx):
    return np.tile(idx.reshape(-1, 16).T, (8, 1)).astype(np.uint16)


def unstriped(offs):
    return offs[:16].T.reshape(-1).astype(np.int64)


E2M1 = np.array([0.0, 0.5, 1.0, 1.5, 2.0, 3.0, 4.0, 6.0, -0.0, -0.5, -1.0, -1.5, -2.0, -3.0, -4.0, -6.0])


def pack_weight(w, fmt):
    k, n = w.shape
    w = f64(np.asarray(w, np.float32).astype(ml_dtypes.bfloat16)).reshape(k // 32, 32, n)
    amax = np.abs(w).max(1)
    if fmt == "e4m3":
        byte = np.frexp(amax)[1] - 1 + 127 - 7
    else:
        mant, ex = np.frexp(amax / 6.0)
        byte = np.where(mant > 0.5, ex, ex - 1) + 127
    byte = np.clip(np.where(amax > 0, byte, 1), 1, 254)
    scaled = (w * np.exp2(127.0 - byte)[:, None, :]).reshape(k, n).astype(np.float32)
    by_word = np.ascontiguousarray(scaled.reshape(k // 512, 128, 4, n).transpose(0, 1, 3, 2))
    if fmt == "e4m3":
        words = by_word.astype(ml_dtypes.float8_e4m3fn).view(np.uint8)
    else:
        c = by_word.astype(ml_dtypes.float4_e2m1fn).view(np.uint8) & 0xF
        words = (c[..., 0::2] | (c[..., 1::2] << 4)).reshape(k // 512, 128, 2 * n)
    return np.ascontiguousarray(words), np.ascontiguousarray(byte.astype(np.uint8).reshape(k // 512, 16, n))


def unpack_weight(words, scales, fmt):
    g, _, n = scales.shape
    words = np.ascontiguousarray(words).reshape(g, 128, n, -1)
    if fmt == "e4m3":
        vals = words.view(ml_dtypes.float8_e4m3fn).astype(np.float64)
    else:
        nib = np.empty((g, 128, n, 4), np.uint8)
        nib[..., 0::2] = words & 0xF
        nib[..., 1::2] = words >> 4
        vals = E2M1[nib]
    vals = vals * np.repeat(np.exp2(scales.astype(np.float64) - 127.0), 8, axis=1)[..., None]
    return vals.transpose(0, 1, 3, 2).reshape(g * 512, n)


def gelu(v):
    return 0.5 * v * (1.0 + np.tanh(np.sqrt(2.0 / np.pi) * (v + 0.044715 * v**3)))


K, T, S, H, T2, P, N = 512, 4096, 1024, 1024, 2048, 1024, 384


def setup_inputs():
    n = np.random.standard_normal
    s = mx_kscale(K)[:, None]
    u = mx_kscale(H)[:, None]
    d = {}
    d["tab_words"], d["tab_scales"] = pack_weight(n((K, T)) * s, "e4m3")
    d["offs"] = striped(np.random.permutation(T)[:S])
    d["offs2"] = striped(np.random.permutation(T2)[:S])
    d["offs3"] = striped(np.random.permutation(T2)[:P])
    d["offs4"] = striped(np.random.permutation(T2)[:P])
    d["w1"] = (1.5 * n((K, H)) / (s * K ** 0.5)).astype(np.float32)
    d["w2_words"], d["w2_scales"] = pack_weight(1.5 * n((K, H)) / (s * K ** 0.5), "e2m1")
    d["w3"] = (1.5 * n((K, H)) / (s * K ** 0.5)).astype(np.float32)
    d["gain"] = (1.5 * np.exp(0.3 * n(H)) * u[:, 0]).astype(np.float32)
    d["wgs"] = np.exp(0.3 * n((128, S))).astype(np.float32)
    d["page0"] = (0.8 * n((H, T2)) * u).astype(np.float32)
    d["lead"] = (0.6 * n(H) * u[:, 0]).astype(np.float32)
    d["w4"] = (n((H, N)) / (u * H ** 0.5)).astype(np.float32)
    d["cap"] = (0.5 + n((N, P))).astype(np.float32)
    d["wgo"] = np.exp(0.3 * n((128, P))).astype(np.float32)
    d["page1"] = (0.8 * n((N, T2))).astype(np.float32)
    return d


def reference(tab_words, tab_scales, offs, offs2, offs3, offs4, w1, w2_words, w2_scales, w3,
              gain, wgs, page0, lead, w4, cap, wgo, page1):
    v = unpack_weight(tab_words, tab_scales, "e4m3")[:, unstriped(offs)]
    first = mxq(f64(w1), 0, "e4m3").T @ v
    second = unpack_weight(w2_words, w2_scales, "e2m1").T @ v
    third = mxq(f64(w3), 0, "e4m3").T @ v
    h = f64(gain)[:, None] * np.tanh(np.maximum(first, second) - third)
    page = f64(page0).copy()
    page[:, unstriped(offs2)] = np.tile(f64(wgs), (H // 128, 1)) * h
    x = page[:, unstriped(offs3)] + f64(lead)[:, None]
    y = np.minimum(mxq(f64(w4), 0, "e4m3").T @ mxq(x, 0, "e4m3"), f64(cap))
    out = f64(page1).copy()
    out[:, unstriped(offs4)] = np.tile(f64(wgo), (N // 128, 1)) * y
    return out

@@ -1,0 +1,334 @@
+from contextlib import ExitStack
+
+import concourse.mybir as mybir
+from concourse.masks import make_identity
+
+K, T, S, H, T2, PICK, N = 512, 4096, 1024, 1024, 2048, 1024, 384
+FLOPS = 2 * 3 * K * H * S + 2 * H * N * PICK
+
+F32 = mybir.dt.float32
+BF16 = mybir.dt.bfloat16
+I32 = mybir.dt.int32
+U32 = mybir.dt.uint32
+U16 = mybir.dt.uint16
+U8 = mybir.dt.uint8
+FP8X4 = mybir.dt.float8_e4m3fn_x4
+FP4X4 = mybir.dt.float4_e2m1fn_x4
+ALU = mybir.AluOpType
+ACT = mybir.ActivationFunctionType
+
+P = 128
+PACK = 4
+PASS = P * PACK
+HALF = 512
+HALF_COLS = HALF // 16
+PASSES = H // PASS
+TILES = H // P
+UNITS = 2 * TILES
+
+
+def tile_list_pane_releading_page_kernel(
+    tc, tab_words, tab_scales, offs, offs2, offs3, offs4, w1, w2_words, w2_scales, w3,
+    gain, wgs, page0, lead, w4, cap, wgo, page1, out,
+):
+    nc = tc.nc
+    with ExitStack() as ctx:
+        held = ctx.enter_context(tc.tile_pool(name="held", bufs=1))
+        ring = ctx.enter_context(tc.tile_pool(name="ring", bufs=2))
+        psum = ctx.enter_context(tc.psum_pool(name="psum", bufs=2))
+
+        def half_list(lst, h):
+            return lst[:, h * HALF_COLS : (h + 1) * HALF_COLS]
+
+        def half_cols(h):
+            return slice(h * HALF, (h + 1) * HALF)
+
+        def load_list(src, name):
+            lst = held.tile([P, S // 16], U16, name=name)
+            nc.sync.dma_start(lst[:], src)
+            return lst
+
+        def load_scale_rows(src, width, name):
+            plane = held.tile([P, width], U8, name=name, tag=name, align_bytes=64)
+            nc.vector.memset(plane[:].bitcast(I32), 0)
+            for q in range(4):
+                nc.gpsimd.dma_start(
+                    plane[32 * q : 32 * q + 4, :].bitcast(I32), src[0, 4 * q : 4 * q + 4, :].bitcast(I32)
+                )
+            return plane
+
+        def load_weight(w, c0):
+            raw = ring.tile([P, PACK, PASS], F32, name="raw", tag="wide", bufs=3)
+            nc.sync.dma_start(raw[:], w[:, c0 : c0 + PASS].rearrange("(p j) c -> p j c", j=PACK))
+            return raw
+
+        def load_page(i):
+            b, t = divmod(i, PACK)
+            page = ring.tile([P, T2], F32, name="page", bufs=6)
+            rows = page0[b * PASS : (b + 1) * PASS, :].rearrange("(p t) m -> p t m", t=PACK)
+            nc.sync.dma_start(page[:], rows[:, t, :])
+            return page
+
+        def load_by_row(src, name):
+            values = held.tile([P, PASSES, PACK], F32, name=name)
+            nc.sync.dma_start(values[:], src.rearrange("(b p t) -> p b t", b=PASSES, t=PACK))
+            return values
+
+        def load_wgs(t0, t1):
+            rows = held.tile([P, t1 - t0, S], F32, name="wgs%d" % t0)
+            for q in range(4):
+                nc.sync.dma_start(
+                    rows[32 * q : 32 * q + 32, :, :], wgs.rearrange("(p t) j -> p t j", t=PACK)[:, t0:t1, :]
+                )
+            return [rows[:, t, :] for t in range(t1 - t0)]
+
+        tab_s = load_scale_rows(tab_scales, T, "tab_s")
+        w2_sraw = load_scale_rows(w2_scales, H, "w2_sraw")
+        ident = held.tile([P, P], F32)
+        make_identity(nc, ident[:])
+        warm_in = held.tile([P, 1], F32)
+        warm_out = held.tile([P, 1], F32)
+        nc.vector.memset(warm_in[:], 0.0)
+        nc.scalar.activation(warm_out[:], warm_in[:], ACT.Tanh)
+
+        list1 = load_list(offs, "list1")
+        w2_raw = held.tile([P, 2 * H], U8, align_bytes=64)
+        nc.sync.dma_start(w2_raw[:].bitcast(I32), w2_words[0].bitcast(I32))
+        w3_raw0 = load_weight(w3, 0)
+        w1_raw0 = load_weight(w1, 0)
+        tab = held.tile([P, T], I32, tag="tab", align_bytes=64)
+        nc.sync.dma_start(tab[:], tab_words[0].rearrange("p t i -> p (t i)").bitcast(I32))
+        list2 = load_list(offs2, "list2")
+        gain_sb = load_by_row(gain, "gain_sb")
+        wgs_sb = load_wgs(0, 1)
+        pages = {0: load_page(0)}
+        list3 = load_list(offs3, "list3")
+        lead_sb = load_by_row(lead, "lead_sb")
+        wgs_sb.extend(load_wgs(1, 2))
+        pages[1] = load_page(1)
+
+        work = [held.tile([P, 2 * HALF], F32, name="work%d" % k, align_bytes=64) for k in range(4)]
+        seconds = [held.tile([P, HALF], F32, name="second_sb%d" % k) for k in range(3)]
+        states = [held.tile([P, HALF], F32, name="state%d" % k) for k in range(2)]
+        planes = held.tile([P, 2, PACK, HALF], BF16)
+
+        def deal_w2(b):
+            words = held.tile([P, 2 * PASS], U8, name="w2_words%d" % b, align_bytes=64)
+            nc.vector.tensor_copy(
+                words[:].rearrange("p (t m e) -> p m t e", t=PACK, e=2),
+                w2_raw[:, 2 * b * PASS : 2 * (b + 1) * PASS].rearrange("p (m t e) -> p m t e", t=PACK, e=2),
+            )
+            scales = held.tile([P, PASS], U8, name="w2_scales%d" % b, align_bytes=64)
+            nc.vector.tensor_copy(
+                scales[:].rearrange("p (t m) -> p m t", t=PACK),
+                w2_sraw[:, b * PASS : (b + 1) * PASS].rearrange("p (m t) -> p m t", t=PACK),
+            )
+            return words, scales
+
+        def grouped_view(k):
+            return work[k][:].bitcast(BF16)
+
+        def round_weight(grouped, raw):
+            for m0 in (0, P // 2):
+                nc.scalar.copy(
+                    grouped.rearrange("p (t m j) -> p m j t", t=PACK, j=PACK)[:, m0 : m0 + P // 2, :, :],
+                    raw[:].rearrange("p j (m t) -> p m j t", t=PACK)[:, m0 : m0 + P // 2, :, :],
+                )
+
+        def quantise(grouped, name, pieces):
+            words = held.tile([P, PASS], U32, name=name + "_words", align_bytes=64)
+            scales = held.tile([P, PASS], U8, name=name + "_scales", align_bytes=64)
+            for c0, c1 in pieces:
+                nc.vector.quantize_mx(
+                    out=words[:, c0:c1].bitcast(FP8X4), scales=scales[:, c0:c1], in_=grouped[:, PACK * c0 : PACK * c1]
+                )
+            return words, scales
+
+        def gather_table(h):
+            scales = held.tile([P, HALF], U8, name="v_scales%d" % h, align_bytes=64)
+            nc.vector.tensor_copy(scales[:], tab_s[:].indirect(half_list(list1, h)))
+            words = held.tile([P, HALF], U32, name="v_words%d" % h, align_bytes=64)
+            nc.vector.tensor_copy(words[:], tab[:].bitcast(U32).indirect(half_list(list1, h)))
+            return words, scales
+
+        whole = [(0, PASS)]
+        w2_q = {b: deal_w2(b) for b in range(PASSES)}
+        round_weight(grouped_view(2), w3_raw0)
+        w3_q = {0: quantise(grouped_view(2), "w3_0", whole)}
+        round_weight(grouped_view(3), w1_raw0)
+        w1_q = {0: quantise(grouped_view(3), "w1_0", whole)}
+        v_q = {h: gather_table(h) for h in range(2)}
+
+        def first_products(u):
+            i, h = divmod(u, 2)
+            b, t = divmod(i, PACK)
+            v_words, v_scales = v_q[h]
+            cols = slice(t * P, (t + 1) * P)
+            banks = []
+            for tag, (words, scales) in (("second", w2_q[b]), ("first", w1_q[b]), ("third", w3_q[b])):
+                bank = psum.tile([P, HALF], F32, name=tag, tag=tag)
+                if tag == "second":
+                    rhs = words[:, 2 * t * P : 2 * (t + 1) * P].bitcast(FP4X4)
+                else:
+                    rhs = words[:, cols].bitcast(FP8X4)
+                for jb in range(HALF // P):
+                    js = slice(jb * P, (jb + 1) * P)
+                    nc.tensor.matmul_mx(
+                        out=bank[:, js], lhsT=v_words[:, js].bitcast(FP8X4), lhsT_scale=v_scales[:, js],
+                        rhs=rhs, rhs_scale=scales[:, cols], start=True, stop=True,
+                    )
+                banks.append(bank)
+            second, first, third = banks
+            nc.scalar.copy(seconds[u % 3][:], second[:])
+            nc.vector.tensor_tensor(work[u % 4][:, half_cols(0)], first[:], seconds[u % 3][:], ALU.max)
+            nc.scalar.activation(work[u % 4][:, half_cols(1)], third[:], ACT.Copy, scale=-1.0)
+
+        def new_state(u):
+            diff = psum.tile([P, HALF], F32)
+            blocks = 2 * HALF // P
+            for k in range(blocks):
+                jb = k % (HALF // P)
+                nc.tensor.matmul(
+                    diff[:, jb * P : (jb + 1) * P], work[u % 4][:, k * P : (k + 1) * P], ident[:],
+                    start=(k == 0), stop=(k == blocks - 1), is_transpose=True,
+                )
+            nc.scalar.activation(states[u % 2][:], diff[:], ACT.Tanh)
+            b, t = divmod(u // 2, PACK)
+            nc.scalar.activation(states[u % 2][:], states[u % 2][:], ACT.Copy, scale=gain_sb[:, b, t : t + 1])
+
+        def put(u):
+            i, h = divmod(u, 2)
+            nc.vector.tensor_tensor(pages[i][:].indirect(half_list(list2, h)), states[u % 2][:], wgs_sb[i % PACK][:, half_cols(h)], ALU.mult)
+
+        def add_lead(dst, picked, i):
+            b, t = divmod(i, PACK)
+            nc.scalar.activation(dst, picked, ACT.Identity, bias=lead_sb[:, b, t : t + 1])
+
+        def interleave(grouped, slot, c0, c1):
+            nc.scalar.copy(
+                grouped[:, PACK * c0 : PACK * c1].rearrange("p (c i t) -> p c t i", i=4, t=PACK),
+                planes[:, slot, :, c0:c1].rearrange("p t (c i) -> p c t i", i=4),
+            )
+
+        x_q = {}
+        later = {}
+
+        def prepare(u):
+            if u == 0:
+                later["w1"] = load_weight(w1, PASS)
+                wgs_sb.extend(load_wgs(2, PACK))
+                pages[2] = load_page(2)
+                later["w3"] = load_weight(w3, PASS)
+                for i in (3, 4, 5):
+                    pages[i] = load_page(i)
+            if u in (1, 3):
+                name, store = ("w1", w1_q) if u == 1 else ("w3", w3_q)
+                round_weight(grouped_view(u), later[name])
+                store[1] = quantise(grouped_view(u), name + "_1", whole)
+            if u in (3, 5):
+                pages[6 + (u - 3) // 2] = load_page(6 + (u - 3) // 2)
+            if u in (5, 7):
+                b = (u - 5) // 2
+                raw = ring.tile([P, PACK, N], F32, name="w4_raw", tag="wide", bufs=3)
+                nc.sync.dma_start(raw[:], w4[b * PASS : (b + 1) * PASS, :].rearrange("(p j) n -> p j n", j=PACK))
+                grouped = grouped_view(u % 4)
+                for n0 in (0, N // 2):
+                    nc.scalar.copy(
+                        grouped[:, PACK * n0 : PACK * (n0 + N // 2)].rearrange("p (c i t) -> p c t i", i=4, t=PACK),
+                        raw[:, :, n0 : n0 + N // 2].rearrange("p t (c i) -> p c t i", i=4),
+                    )
+                later["w4", b] = quantise(grouped, "w4_%d" % b, [(0, 2 * P), (2 * P, N)])
+            if u == 8:
+                later["list4"] = load_list(offs4, "list4")
+                cap_sb = held.tile([P, N // P, PICK], F32, tag="tab", align_bytes=64)
+                nc.sync.dma_start(cap_sb[:], cap.rearrange("(a p) j -> p a j", p=P))
+                later["cap"] = cap_sb
+                wgo_sb = held.tile([P, PICK], F32, tag="tab_s", align_bytes=64)
+                nc.sync.dma_start(wgo_sb[:], wgo)
+                later["wgo"] = wgo_sb
+                for a in range(N // P):
+                    sheet = ring.tile([P, T2], F32, name="sheet", tag="wide", bufs=3)
+                    nc.sync.dma_start(sheet[:], page1[a * P : (a + 1) * P, :])
+                    later["sheet", a] = sheet
+            if u in (9, 11):
+                h = (u - 9) // 2
+                grouped = grouped_view(u % 4)
+                for c0 in (0, HALF // 2):
+                    interleave(grouped, h, c0, c0 + HALF // 2)
+                x_q[0, h] = quantise(grouped, "x_0_%d" % h, whole)
+
+        first_products(0)
+        for u in range(UNITS):
+            if u + 1 < UNITS:
+                first_products(u + 1)
+            new_state(u)
+            if u >= 2 and u % 2 == 0:
+                i = u // 2 - 1
+                if i < PACK:
+                    nc.vector.tensor_copy(work[u % 4][:], pages[i][:].indirect(list3[:]))
+                else:
+                    nc.vector.tensor_copy(work[u % 4][:, half_cols(0)], pages[i][:].indirect(half_list(list3, 0)))
+            put(u)
+            if u >= 3 and u % 2 == 1:
+                i = (u - 3) // 2
+                if i < PACK:
+                    add_lead(planes[:, :, i, :], work[(u - 1) % 4][:].rearrange("p (h j) -> p h j", h=2), i)
+                else:
+                    add_lead(planes[:, 0, i - PACK, :], work[(u - 1) % 4][:, half_cols(0)], i)
+            prepare(u)
+
+        last = UNITS - 1
+        picked_last = work[0][:, half_cols(0)]
+        nc.vector.tensor_copy(picked_last, pages[TILES - 1][:].indirect(half_list(list3, 0)))
+        add_lead(planes[:, 0, PACK - 1, :], picked_last, TILES - 1)
+        grouped_a = grouped_view(1)
+        interleave(grouped_a, 0, 0, HALF)
+        targets = [states[last % 2][:], wgs_sb[PACK - 1][:, half_cols(1)], picked_last]
+        for t in range(PACK - 1):
+            nc.vector.tensor_copy(targets[t], pages[PACK + t][:].indirect(half_list(list3, 1)))
+        x_q[1, 0] = quantise(grouped_a, "x_1_0", whole)
+        targets.append(work[1][:, half_cols(0)])
+        nc.vector.tensor_copy(targets[-1], pages[TILES - 1][:].indirect(half_list(list3, 1)))
+        for t in range(PACK):
+            add_lead(planes[:, 0, t, :], targets[t], PACK + t)
+        grouped_b = grouped_view(3)
+        interleave(grouped_b, 0, 0, HALF)
+
+        def last_product(a, h):
+            bank = psum.tile([P, HALF], F32, name="product", tag=("second", "first", "third")[a])
+            for b in range(PASSES):
+                cols = slice(a * P, (a + 1) * P)
+                w4_words, w4_scales = later["w4", b]
+                x_words, x_scales = x_q[b, h]
+                nc.tensor.matmul_mx(
+                    out=bank[:], lhsT=w4_words[:, cols].bitcast(FP8X4), lhsT_scale=w4_scales[:, cols],
+                    rhs=x_words[:].bitcast(FP8X4), rhs_scale=x_scales[:], start=(b == 0), stop=(b == PASSES - 1),
+                )
+            return bank
+
+        def cap_it(low, bank, a, h):
+            nc.vector.tensor_tensor(low, bank[:], later["cap"][:, a, half_cols(h)], ALU.min)
+
+        def place(low, a, h):
+            sheet = later["sheet", a]
+            nc.vector.tensor_tensor(
+                sheet[:].indirect(half_list(later["list4"], h)), low, later["wgo"][:, half_cols(h)], ALU.mult
+            )
+            if h == 1:
+                nc.sync.dma_start(out[a * P : (a + 1) * P, :], sheet[:])
+
+        banks = [last_product(a, 0) for a in range(N // P)]
+        for a in range(2):
+            cap_it(work[2][:, half_cols(a)], banks[a], a, 0)
+        for a in range(2):
+            place(work[2][:, half_cols(a)], a, 0)
+        x_q[1, 1] = quantise(grouped_b, "x_1_1", whole)
+        low = work[3][:, half_cols(0)]
+        cap_it(low, banks[2], 2, 0)
+        place(low, 2, 0)
+        lows = [work[2][:, half_cols(0)], work[2][:, half_cols(1)], work[0][:, half_cols(1)]]
+        banks = [last_product(a, 1) for a in range(N // P)]
+        for a in range(N // P):
+            cap_it(lows[a], banks[a], a, 1)
+        for a in range(N // P):
+            place(lows[a], a, 1)

@@ -25,6 +25,11 @@ HALF_COLS = HALF // 16
 PASSES = H // PASS
 TILES = H // P
 UNITS = 2 * TILES
+FETCH_LAG = 3
+PLANE_LAG = FETCH_LAG + 1
+ROOMS = UNITS - 1
+TURNS = 6
+UPRIGHT = 2
 
 
 def tile_list_pane_releading_page_kernel(
@@ -35,7 +40,9 @@ def tile_list_pane_releading_page_kernel(
     with ExitStack() as ctx:
         held = ctx.enter_context(tc.tile_pool(name="held", bufs=1))
         ring = ctx.enter_context(tc.tile_pool(name="ring", bufs=2))
+        shared = ctx.enter_context(tc.tile_pool(name="shared", bufs=1))
         psum = ctx.enter_context(tc.psum_pool(name="psum", bufs=2))
+        turns = ctx.enter_context(tc.psum_pool(name="turns", bufs=1))
 
         def half_list(lst, h):
             return lst[:, h * HALF_COLS : (h + 1) * HALF_COLS]
@@ -49,17 +56,18 @@ def tile_list_pane_releading_page_kernel(
             return lst
 
         def load_scale_rows(src, width, name):
-            plane = held.tile([P, width], U8, name=name, tag=name, align_bytes=64)
-            nc.vector.memset(plane[:].bitcast(I32), 0)
+            rows = held.tile([P, width // 4], I32, name=name)
             for q in range(4):
-                nc.gpsimd.dma_start(
-                    plane[32 * q : 32 * q + 4, :].bitcast(I32), src[0, 4 * q : 4 * q + 4, :].bitcast(I32)
-                )
-            return plane
+                nc.sync.dma_start(rows[32 * q : 32 * q + 4, :], src[0, 4 * q : 4 * q + 4, :].bitcast(I32))
+            return rows
 
-        def load_weight(w, c0):
-            raw = ring.tile([P, PACK, PASS], F32, name="raw", tag="wide", bufs=3)
-            nc.sync.dma_start(raw[:], w[:, c0 : c0 + PASS].rearrange("(p j) c -> p j c", j=PACK))
+        def fill_plane(plane, rows):
+            for q in range(4):
+                nc.vector.tensor_copy(plane[32 * q : 32 * q + 4, :].bitcast(I32), rows[32 * q : 32 * q + 4, :])
+
+        def load_weight(w, c0, width=PASS, pool=ring, tag="wide", bufs=3):
+            raw = pool.tile([P, PACK, width], F32, name="raw", tag=tag, bufs=bufs, align_bytes=64)
+            nc.sync.dma_start(raw[:], w[:, c0 : c0 + width].rearrange("(p j) c -> p j c", j=PACK))
             return raw
 
         def load_page(i):
@@ -82,10 +90,10 @@ def tile_list_pane_releading_page_kernel(
                 )
             return [rows[:, t, :] for t in range(t1 - t0)]
 
-        tab_s = load_scale_rows(tab_scales, T, "tab_s")
-        w2_sraw = load_scale_rows(w2_scales, H, "w2_sraw")
         ident = held.tile([P, P], F32)
         make_identity(nc, ident[:])
+        tab_s = held.tile([P, T], U8, align_bytes=64)
+        nc.vector.memset(tab_s[:].bitcast(I32), 0)
         warm_in = held.tile([P, 1], F32)
         warm_out = held.tile([P, 1], F32)
         nc.vector.memset(warm_in[:], 0.0)
@@ -94,211 +102,277 @@ def tile_list_pane_releading_page_kernel(
         list1 = load_list(offs, "list1")
         w2_raw = held.tile([P, 2 * H], U8, align_bytes=64)
         nc.sync.dma_start(w2_raw[:].bitcast(I32), w2_words[0].bitcast(I32))
-        w3_raw0 = load_weight(w3, 0)
-        w1_raw0 = load_weight(w1, 0)
-        tab = held.tile([P, T], I32, tag="tab", align_bytes=64)
+        tab_rows = load_scale_rows(tab_scales, T, "tab_rows")
+        tab = shared.tile([P, T], I32, offset=0, align_bytes=64)
         nc.sync.dma_start(tab[:], tab_words[0].rearrange("p t i -> p (t i)").bitcast(I32))
+        w1_raw0 = load_weight(w1, 0)
+        w2_rows = load_scale_rows(w2_scales, H, "w2_rows")
+        w3_head = [load_weight(w3, k * PASS // 2, PASS // 2, held, "w3_head%d" % k, 1) for k in range(2)]
         list2 = load_list(offs2, "list2")
         gain_sb = load_by_row(gain, "gain_sb")
-        wgs_sb = load_wgs(0, 1)
         pages = {0: load_page(0)}
-        list3 = load_list(offs3, "list3")
+        wgs_sb = load_wgs(0, 1)
         lead_sb = load_by_row(lead, "lead_sb")
+        list3 = load_list(offs3, "list3")
         wgs_sb.extend(load_wgs(1, 2))
         pages[1] = load_page(1)
 
-        work = [held.tile([P, 2 * HALF], F32, name="work%d" % k, align_bytes=64) for k in range(4)]
+        larger = [held.tile([P, HALF], F32, name="larger%d" % k, align_bytes=64) for k in range(4)]
         seconds = [held.tile([P, HALF], F32, name="second_sb%d" % k) for k in range(3)]
-        states = [held.tile([P, HALF], F32, name="state%d" % k) for k in range(2)]
-        planes = held.tile([P, 2, PACK, HALF], BF16)
+        side = [held.tile([P, HALF], F32, name="side%d" % k) for k in range(3)]
+        state = [held.tile([P, HALF], F32, name="state%d" % k) for k in range(3)]
+        rooms = held.tile([P, ROOMS, HALF], F32, align_bytes=64)
+        turn = [turns.tile([P, HALF], F32, name="turn%d" % k) for k in range(TURNS)]
 
-        def deal_w2(b):
+        def room_index(u):
+            return (u - PLANE_LAG) % ROOMS
+
+        def plane_of(f):
+            return rooms[:].bitcast(BF16)[:, room_index(f + PLANE_LAG), 0:HALF]
+
+        def planes_of(b, h):
+            first = room_index(2 * PACK * b + h + PLANE_LAG)
+            return rooms[:].bitcast(BF16)[:, first : first + 2 * PACK - 1 : 2, 0:HALF]
+
+        low_half, high_half = half_cols(0), half_cols(1)
+
+        def deal_words(b):
             words = held.tile([P, 2 * PASS], U8, name="w2_words%d" % b, align_bytes=64)
             nc.vector.tensor_copy(
                 words[:].rearrange("p (t m e) -> p m t e", t=PACK, e=2),
                 w2_raw[:, 2 * b * PASS : 2 * (b + 1) * PASS].rearrange("p (m t e) -> p m t e", t=PACK, e=2),
             )
+            return words
+
+        def deal_scales(b, plane):
             scales = held.tile([P, PASS], U8, name="w2_scales%d" % b, align_bytes=64)
             nc.vector.tensor_copy(
                 scales[:].rearrange("p (t m) -> p m t", t=PACK),
-                w2_sraw[:, b * PASS : (b + 1) * PASS].rearrange("p (m t) -> p m t", t=PACK),
+                plane[:, b * PASS : (b + 1) * PASS].rearrange("p (m t) -> p m t", t=PACK),
             )
-            return words, scales
+            return scales
 
-        def grouped_view(k):
-            return work[k][:].bitcast(BF16)
+        def round_weight(copy, grouped, raw, k):
+            copy(
+                grouped.rearrange("p (t m j) -> p m j t", t=PACK, j=PACK)[:, k * P // 2 : (k + 1) * P // 2, :, :],
+                raw.rearrange("p j (m t) -> p m j t", t=PACK),
+            )
 
-        def round_weight(grouped, raw):
-            for m0 in (0, P // 2):
-                nc.scalar.copy(
-                    grouped.rearrange("p (t m j) -> p m j t", t=PACK, j=PACK)[:, m0 : m0 + P // 2, :, :],
-                    raw[:].rearrange("p j (m t) -> p m j t", t=PACK)[:, m0 : m0 + P // 2, :, :],
-                )
+        def halves_of(raw):
+            return [raw[:, :, k * PASS // 2 : (k + 1) * PASS // 2] for k in range(2)]
 
-        def quantise(grouped, name, pieces):
-            words = held.tile([P, PASS], U32, name=name + "_words", align_bytes=64)
+        def mx_tiles(name, pool=held, words_at=None):
+            words = pool.tile([P, PASS], U32, name=name + "_words", offset=words_at, align_bytes=64)
             scales = held.tile([P, PASS], U8, name=name + "_scales", align_bytes=64)
-            for c0, c1 in pieces:
-                nc.vector.quantize_mx(
-                    out=words[:, c0:c1].bitcast(FP8X4), scales=scales[:, c0:c1], in_=grouped[:, PACK * c0 : PACK * c1]
-                )
             return words, scales
 
-        def gather_table(h):
-            scales = held.tile([P, HALF], U8, name="v_scales%d" % h, align_bytes=64)
-            nc.vector.tensor_copy(scales[:], tab_s[:].indirect(half_list(list1, h)))
-            words = held.tile([P, HALF], U32, name="v_words%d" % h, align_bytes=64)
-            nc.vector.tensor_copy(words[:], tab[:].bitcast(U32).indirect(half_list(list1, h)))
-            return words, scales
+        def quantise(target, c0, c1, grouped):
+            words, scales = target
+            nc.vector.quantize_mx(out=words[:, c0:c1].bitcast(FP8X4), scales=scales[:, c0:c1], in_=grouped)
 
-        whole = [(0, PASS)]
-        w2_q = {b: deal_w2(b) for b in range(PASSES)}
-        round_weight(grouped_view(2), w3_raw0)
-        w3_q = {0: quantise(grouped_view(2), "w3_0", whole)}
-        round_weight(grouped_view(3), w1_raw0)
-        w1_q = {0: quantise(grouped_view(3), "w1_0", whole)}
-        v_q = {h: gather_table(h) for h in range(2)}
+        w2_dealt = [deal_words(b) for b in range(PASSES)]
+        fill_plane(tab_s, tab_rows)
+        v_scales = held.tile([P, S], U8, align_bytes=64)
+        nc.vector.tensor_copy(v_scales[:], tab_s[:].indirect(list1[:]))
+        v_words = held.tile([P, S], U32, align_bytes=64)
+        nc.vector.tensor_copy(v_words[:], tab[:].bitcast(U32).indirect(list1[:]))
+        v_q = [(v_words[:, half_cols(h)], v_scales[:, half_cols(h)]) for h in range(2)]
+        w2_plane = shared.tile([P, H], U8, offset=0, align_bytes=64)
+        nc.vector.memset(w2_plane[:].bitcast(I32), 0)
+        fill_plane(w2_plane, w2_rows)
+        w2_q = [(w2_dealt[b], deal_scales(b, w2_plane)) for b in range(PASSES)]
+        w1_grouped = rooms[:, 0:2, :].rearrange("p r c -> p (r c)").bitcast(BF16)
+        w1_halves = halves_of(w1_raw0)
+        for k in range(2):
+            round_weight(nc.scalar.copy, w1_grouped, w1_halves[k], k)
+        w3_grouped = shared.tile([P, PACK * PASS], BF16, offset=H, align_bytes=64)
+        round_weight(nc.scalar.copy, w3_grouped[:], w3_head[0][:], 0)
+        round_weight(nc.vector.tensor_copy, w3_grouped[:], w3_head[1][:], 1)
+        w1_q = [mx_tiles("w1_0", shared, H + 2 * PACK * PASS), mx_tiles("w1_1")]
+        w3_q = [mx_tiles("w3_0"), mx_tiles("w3_1")]
+        quantise(w1_q[0], 0, PASS, w1_grouped)
+        for c0, c1 in ((0, P), (P, 2 * P), (2 * P, PASS)):
+            quantise(w3_q[0], c0, c1, w3_grouped[:, PACK * c0 : PACK * c1])
 
         def first_products(u):
             i, h = divmod(u, 2)
             b, t = divmod(i, PACK)
-            v_words, v_scales = v_q[h]
+            v_w, v_s = v_q[h]
             cols = slice(t * P, (t + 1) * P)
             banks = []
             for tag, (words, scales) in (("second", w2_q[b]), ("first", w1_q[b]), ("third", w3_q[b])):
-                bank = psum.tile([P, HALF], F32, name=tag, tag=tag)
+                if tag == "first":
+                    bank = psum.tile([P, HALF], F32, name=tag, tag=tag)
+                else:
+                    bank = turn[(u - (3 if tag == "second" else 1)) % TURNS]
                 if tag == "second":
                     rhs = words[:, 2 * t * P : 2 * (t + 1) * P].bitcast(FP4X4)
                 else:
                     rhs = words[:, cols].bitcast(FP8X4)
-                for jb in range(HALF // P):
+                if u < UPRIGHT:
+                    nc.tensor.matmul_mx(
+                        out=bank[:], lhsT=rhs, lhsT_scale=scales[:, cols],
+                        rhs=v_w.bitcast(FP8X4), rhs_scale=v_s, start=True, stop=True,
+                    )
+                for jb in range(HALF // P if u >= UPRIGHT else 0):
                     js = slice(jb * P, (jb + 1) * P)
                     nc.tensor.matmul_mx(
-                        out=bank[:, js], lhsT=v_words[:, js].bitcast(FP8X4), lhsT_scale=v_scales[:, js],
+                        out=bank[:, js], lhsT=v_w[:, js].bitcast(FP8X4), lhsT_scale=v_s[:, js],
                         rhs=rhs, rhs_scale=scales[:, cols], start=True, stop=True,
                     )
                 banks.append(bank)
             second, first, third = banks
-            nc.scalar.copy(seconds[u % 3][:], second[:])
-            nc.vector.tensor_tensor(work[u % 4][:, half_cols(0)], first[:], seconds[u % 3][:], ALU.max)
-            nc.scalar.activation(work[u % 4][:, half_cols(1)], third[:], ACT.Copy, scale=-1.0)
+            second_sb, big, room = seconds[u % 3][:], larger[u % 4][:], rooms[:, room_index(u), :]
+            nc.scalar.copy(second_sb, second[:])
+            nc.vector.tensor_tensor(big, first[:], second_sb, ALU.max)
+            if u < UPRIGHT:
+                nc.vector.tensor_tensor(room, big, third[:], ALU.subtract)
+            else:
+                nc.scalar.activation(room, third[:], ACT.Copy, scale=-1.0)
 
         def new_state(u):
-            diff = psum.tile([P, HALF], F32)
-            blocks = 2 * HALF // P
-            for k in range(blocks):
-                jb = k % (HALF // P)
-                nc.tensor.matmul(
-                    diff[:, jb * P : (jb + 1) * P], work[u % 4][:, k * P : (k + 1) * P], ident[:],
-                    start=(k == 0), stop=(k == blocks - 1), is_transpose=True,
-                )
-            nc.scalar.activation(states[u % 2][:], diff[:], ACT.Tanh)
+            room = rooms[:, room_index(u), :]
+            if u < UPRIGHT:
+                diff = room
+            else:
+                diff = turn[u % TURNS][:]
+                blocks = [(src, jb) for src in (larger[u % 4][:], room) for jb in range(HALF // P)]
+                for k, (src, jb) in enumerate(blocks):
+                    js = slice(jb * P, (jb + 1) * P)
+                    nc.tensor.matmul(
+                        diff[:, js], src[:, js], ident[:], start=(k == 0), stop=(k == len(blocks) - 1), is_transpose=True
+                    )
+            nc.scalar.activation(side[u % 3][:], diff, ACT.Tanh)
+
+        def apply_gain(u):
             b, t = divmod(u // 2, PACK)
-            nc.scalar.activation(states[u % 2][:], states[u % 2][:], ACT.Copy, scale=gain_sb[:, b, t : t + 1])
+            nc.scalar.activation(state[u % 3][:], side[u % 3][:], ACT.Copy, scale=gain_sb[:, b, t : t + 1])
 
         def put(u):
             i, h = divmod(u, 2)
-            nc.vector.tensor_tensor(pages[i][:].indirect(half_list(list2, h)), states[u % 2][:], wgs_sb[i % PACK][:, half_cols(h)], ALU.mult)
+            nc.vector.tensor_tensor(
+                pages[i][:].indirect(half_list(list2, h)), state[u % 3][:], wgs_sb[i % PACK][:, half_cols(h)], ALU.mult
+            )
+
+        def fetch(dst, i, h):
+            nc.vector.tensor_copy(dst, pages[i][:].indirect(half_list(list3, h)))
 
         def add_lead(dst, picked, i):
             b, t = divmod(i, PACK)
             nc.scalar.activation(dst, picked, ACT.Identity, bias=lead_sb[:, b, t : t + 1])
 
-        def interleave(grouped, slot, c0, c1):
+        def interleave(grouped, planes, c0, c1):
             nc.scalar.copy(
-                grouped[:, PACK * c0 : PACK * c1].rearrange("p (c i t) -> p c t i", i=4, t=PACK),
-                planes[:, slot, :, c0:c1].rearrange("p t (c i) -> p c t i", i=4),
+                grouped.rearrange("p (c i t) -> p c t i", i=4, t=PACK),
+                planes[:, :, c0:c1].rearrange("p t (c i) -> p c t i", i=4),
             )
 
-        x_q = {}
+        x_q = {(b, h): mx_tiles("x_%d_%d" % (b, h)) for b in range(PASSES) for h in range(2)}
+        w4_q = [mx_tiles("w4_%d" % b) for b in range(PASSES)]
         later = {}
+
+        def weight_piece(room, raw, target, k):
+            nc.scalar.copy(
+                room.rearrange("p (t m j) -> p m j t", t=2, j=PACK),
+                raw[:].rearrange("p j (m t) -> p m j t", t=PACK)[:, :, :, 2 * k : 2 * k + 2],
+            )
+            quantise(target, 2 * k * P, 2 * (k + 1) * P, room)
+
+        def w4_piece(room, b, n0, n1):
+            nc.scalar.copy(
+                room.rearrange("p (c i t) -> p c t i", i=4, t=PACK),
+                later["w4", b][:, :, n0:n1].rearrange("p t (c i) -> p c t i", i=4),
+            )
+            quantise(w4_q[b], n0, n1, room)
+
+        def side_job(u, room):
+            if 1 <= u <= 4:
+                k, which = divmod(u - 1, 2)
+                weight_piece(room, later[("w1", "w3")[which]], (w1_q, w3_q)[which][1], k)
+            elif u in (5, 6):
+                w4_piece(room, u - 5, 0, 2 * P)
+            elif u == 7:
+                for b in range(PASSES):
+                    w4_piece(room[:, b * PASS : (b + 1) * PASS], b, 2 * P, N)
+            elif 11 <= u <= 14:
+                h, k = divmod(u - 11, 2)
+                c0, c1 = k * HALF // 2, (k + 1) * HALF // 2
+                interleave(room, planes_of(0, h), c0, c1)
+                quantise(x_q[0, h], c0, c1, room)
 
         def prepare(u):
             if u == 0:
                 later["w1"] = load_weight(w1, PASS)
-                wgs_sb.extend(load_wgs(2, PACK))
-                pages[2] = load_page(2)
                 later["w3"] = load_weight(w3, PASS)
-                for i in (3, 4, 5):
+                wgs_sb.extend(load_wgs(2, PACK))
+                for i in (2, 3, 4, 5):
                     pages[i] = load_page(i)
-            if u in (1, 3):
-                name, store = ("w1", w1_q) if u == 1 else ("w3", w3_q)
-                round_weight(grouped_view(u), later[name])
-                store[1] = quantise(grouped_view(u), name + "_1", whole)
-            if u in (3, 5):
-                pages[6 + (u - 3) // 2] = load_page(6 + (u - 3) // 2)
-            if u in (5, 7):
-                b = (u - 5) // 2
-                raw = ring.tile([P, PACK, N], F32, name="w4_raw", tag="wide", bufs=3)
+            if u in (4, 6):
+                pages[6 + (u - 4) // 2] = load_page(6 + (u - 4) // 2)
+            if u in (3, 4):
+                b = u - 3
+                raw = ring.tile([P, PACK, N], F32, name="w4_raw", tag="wide", bufs=3, align_bytes=64)
                 nc.sync.dma_start(raw[:], w4[b * PASS : (b + 1) * PASS, :].rearrange("(p j) n -> p j n", j=PACK))
-                grouped = grouped_view(u % 4)
-                for n0 in (0, N // 2):
-                    nc.scalar.copy(
-                        grouped[:, PACK * n0 : PACK * (n0 + N // 2)].rearrange("p (c i t) -> p c t i", i=4, t=PACK),
-                        raw[:, :, n0 : n0 + N // 2].rearrange("p t (c i) -> p c t i", i=4),
-                    )
-                later["w4", b] = quantise(grouped, "w4_%d" % b, [(0, 2 * P), (2 * P, N)])
+                later["w4", b] = raw
             if u == 8:
                 later["list4"] = load_list(offs4, "list4")
-                cap_sb = held.tile([P, N // P, PICK], F32, tag="tab", align_bytes=64)
+                cap_sb = held.tile([P, N // P, PICK], F32)
                 nc.sync.dma_start(cap_sb[:], cap.rearrange("(a p) j -> p a j", p=P))
                 later["cap"] = cap_sb
-                wgo_sb = held.tile([P, PICK], F32, tag="tab_s", align_bytes=64)
+                wgo_sb = held.tile([P, PICK], F32)
                 nc.sync.dma_start(wgo_sb[:], wgo)
                 later["wgo"] = wgo_sb
                 for a in range(N // P):
-                    sheet = ring.tile([P, T2], F32, name="sheet", tag="wide", bufs=3)
+                    sheet = ring.tile([P, T2], F32, name="sheet", tag="wide", bufs=3, align_bytes=64)
                     nc.sync.dma_start(sheet[:], page1[a * P : (a + 1) * P, :])
                     later["sheet", a] = sheet
-            if u in (9, 11):
-                h = (u - 9) // 2
-                grouped = grouped_view(u % 4)
-                for c0 in (0, HALF // 2):
-                    interleave(grouped, h, c0, c0 + HALF // 2)
-                x_q[0, h] = quantise(grouped, "x_0_%d" % h, whole)
+
+        def fetched_at(u):
+            i, h = divmod(u - FETCH_LAG, 2)
+            return 0 <= i and (i < PACK or h == 0)
 
         first_products(0)
-        for u in range(UNITS):
+        for u in range(UNITS + 1):
             if u + 1 < UNITS:
                 first_products(u + 1)
-            new_state(u)
-            if u >= 2 and u % 2 == 0:
-                i = u // 2 - 1
-                if i < PACK:
-                    nc.vector.tensor_copy(work[u % 4][:], pages[i][:].indirect(list3[:]))
-                else:
-                    nc.vector.tensor_copy(work[u % 4][:, half_cols(0)], pages[i][:].indirect(half_list(list3, 0)))
-            put(u)
-            if u >= 3 and u % 2 == 1:
-                i = (u - 3) // 2
-                if i < PACK:
-                    add_lead(planes[:, :, i, :], work[(u - 1) % 4][:].rearrange("p (h j) -> p h j", h=2), i)
-                else:
-                    add_lead(planes[:, 0, i - PACK, :], work[(u - 1) % 4][:, half_cols(0)], i)
-            prepare(u)
+            if u < UNITS:
+                new_state(u)
+                apply_gain(u)
+            if fetched_at(u - 1):
+                f = u - 1 - FETCH_LAG
+                add_lead(plane_of(f), side[(u - 1) % 3][:], f // 2)
+            if u < UNITS:
+                if fetched_at(u):
+                    fetch(side[u % 3][:], *divmod(u - FETCH_LAG, 2))
+                put(u)
+                side_job(u, larger[u % 4][:].bitcast(BF16))
+                prepare(u)
 
         last = UNITS - 1
-        picked_last = work[0][:, half_cols(0)]
-        nc.vector.tensor_copy(picked_last, pages[TILES - 1][:].indirect(half_list(list3, 0)))
-        add_lead(planes[:, 0, PACK - 1, :], picked_last, TILES - 1)
-        grouped_a = grouped_view(1)
-        interleave(grouped_a, 0, 0, HALF)
-        targets = [states[last % 2][:], wgs_sb[PACK - 1][:, half_cols(1)], picked_last]
+        spare = [rooms[:, 2 * k : 2 * k + 2, :].rearrange("p r c -> p (r c)") for k in range(3)]
+        tile_c, tile_a, tile_b = spare
+        picked_last = side[(last + 1) % 3][:]
+        planes = planes_of(1, 0)
+        fetch(picked_last, TILES - 1, 0)
+        add_lead(planes[:, PACK - 1, :], picked_last, TILES - 1)
+        grouped_a = tile_c.bitcast(BF16)
+        interleave(grouped_a, planes, 0, HALF)
+        targets = [state[last % 3][:], wgs_sb[PACK - 1][:, high_half], picked_last]
         for t in range(PACK - 1):
-            nc.vector.tensor_copy(targets[t], pages[PACK + t][:].indirect(half_list(list3, 1)))
-        x_q[1, 0] = quantise(grouped_a, "x_1_0", whole)
-        targets.append(work[1][:, half_cols(0)])
-        nc.vector.tensor_copy(targets[-1], pages[TILES - 1][:].indirect(half_list(list3, 1)))
+            fetch(targets[t], PACK + t, 1)
+        quantise(x_q[1, 0], 0, PASS, grouped_a)
+        targets.append(tile_c[:, low_half])
+        fetch(targets[-1], TILES - 1, 1)
         for t in range(PACK):
-            add_lead(planes[:, 0, t, :], targets[t], PACK + t)
-        grouped_b = grouped_view(3)
-        interleave(grouped_b, 0, 0, HALF)
+            add_lead(planes[:, t, :], targets[t], PACK + t)
+        grouped_b = tile_a.bitcast(BF16)
+        interleave(grouped_b, planes, 0, HALF)
 
         def last_product(a, h):
-            bank = psum.tile([P, HALF], F32, name="product", tag=("second", "first", "third")[a])
+            bank = turn[h * (N // P) + a]
             for b in range(PASSES):
                 cols = slice(a * P, (a + 1) * P)
-                w4_words, w4_scales = later["w4", b]
+                w4_words, w4_scales = w4_q[b]
                 x_words, x_scales = x_q[b, h]
                 nc.tensor.matmul_mx(
                     out=bank[:], lhsT=w4_words[:, cols].bitcast(FP8X4), lhsT_scale=w4_scales[:, cols],
@@ -319,14 +393,14 @@ def tile_list_pane_releading_page_kernel(
 
         banks = [last_product(a, 0) for a in range(N // P)]
         for a in range(2):
-            cap_it(work[2][:, half_cols(a)], banks[a], a, 0)
+            cap_it(tile_b[:, half_cols(a)], banks[a], a, 0)
         for a in range(2):
-            place(work[2][:, half_cols(a)], a, 0)
-        x_q[1, 1] = quantise(grouped_b, "x_1_1", whole)
-        low = work[3][:, half_cols(0)]
+            place(tile_b[:, half_cols(a)], a, 0)
+        quantise(x_q[1, 1], 0, PASS, grouped_b)
+        low = tile_a[:, low_half]
         cap_it(low, banks[2], 2, 0)
         place(low, 2, 0)
-        lows = [work[2][:, half_cols(0)], work[2][:, half_cols(1)], work[0][:, half_cols(1)]]
+        lows = [tile_b[:, low_half], tile_b[:, high_half], larger[0][:]]
         banks = [last_product(a, 1) for a in range(N // P)]
         for a in range(N // P):
             cap_it(lows[a], banks[a], a, 1)

@@ -28,7 +28,10 @@ UNITS = 2 * TILES
 FETCH_LAG = 3
 PLANE_LAG = FETCH_LAG + 1
 ROOMS = UNITS - 1
-TURNS = 6
+TURNS = 3
+J0 = 3
+WL = 1
+AHEAD = 8
 UPRIGHT = 2
 
 
@@ -92,8 +95,10 @@ def tile_list_pane_releading_page_kernel(
 
         ident = held.tile([P, P], F32)
         make_identity(nc, ident[:])
-        tab_s = held.tile([P, T], U8, align_bytes=64)
+        tab_s = shared.tile([P, T], U8, offset=0, align_bytes=64)
         nc.vector.memset(tab_s[:].bitcast(I32), 0)
+        w2_plane = held.tile([P, H], U8, align_bytes=64)
+        nc.vector.memset(w2_plane[:].bitcast(I32), 0)
         warm_in = held.tile([P, 1], F32)
         warm_out = held.tile([P, 1], F32)
         nc.vector.memset(warm_in[:], 0.0)
@@ -103,26 +108,27 @@ def tile_list_pane_releading_page_kernel(
         w2_raw = held.tile([P, 2 * H], U8, align_bytes=64)
         nc.sync.dma_start(w2_raw[:].bitcast(I32), w2_words[0].bitcast(I32))
         tab_rows = load_scale_rows(tab_scales, T, "tab_rows")
-        tab = shared.tile([P, T], I32, offset=0, align_bytes=64)
-        nc.sync.dma_start(tab[:], tab_words[0].rearrange("p t i -> p (t i)").bitcast(I32))
-        w1_raw0 = load_weight(w1, 0)
+        w1_head = [load_weight(w1, k * PASS // 2, PASS // 2, held, "w1_head%d" % k, 1) for k in range(2)]
         w2_rows = load_scale_rows(w2_scales, H, "w2_rows")
-        w3_head = [load_weight(w3, k * PASS // 2, PASS // 2, held, "w3_head%d" % k, 1) for k in range(2)]
+        tab = shared.tile([P, T], I32, offset=T, align_bytes=64)
+        nc.sync.dma_start(tab[:], tab_words[0].rearrange("p t i -> p (t i)").bitcast(I32))
+        seconds_all = held.tile([P, 4, HALF], F32)
+        nc.sync.dma_start(seconds_all[:], w3[:, 0:PASS].rearrange("(p j) c -> p j c", j=PACK))
+        w3_head = [seconds_all[:, :, k * PASS // 2 : (k + 1) * PASS // 2] for k in range(2)]
         list2 = load_list(offs2, "list2")
         gain_sb = load_by_row(gain, "gain_sb")
         pages = {0: load_page(0)}
         wgs_sb = load_wgs(0, 1)
         lead_sb = load_by_row(lead, "lead_sb")
         list3 = load_list(offs3, "list3")
-        wgs_sb.extend(load_wgs(1, 2))
-        pages[1] = load_page(1)
 
-        larger = [held.tile([P, HALF], F32, name="larger%d" % k, align_bytes=64) for k in range(4)]
-        seconds = [held.tile([P, HALF], F32, name="second_sb%d" % k) for k in range(3)]
-        side = [held.tile([P, HALF], F32, name="side%d" % k) for k in range(3)]
+        larger_all = held.tile([P, 4, HALF], F32, align_bytes=64)
+        larger = [larger_all[:, k, :] for k in range(4)]
+        side = [held.tile([P, HALF], F32, name="side%d" % k, align_bytes=64) for k in range(3)]
         state = [held.tile([P, HALF], F32, name="state%d" % k) for k in range(3)]
         rooms = held.tile([P, ROOMS, HALF], F32, align_bytes=64)
         turn = [turns.tile([P, HALF], F32, name="turn%d" % k) for k in range(TURNS)]
+        extra = [turns.tile([P, HALF], F32, name="extra%d" % k) for k in range(N // P)]
 
         def room_index(u):
             return (u - PLANE_LAG) % ROOMS
@@ -152,14 +158,12 @@ def tile_list_pane_releading_page_kernel(
             )
             return scales
 
-        def round_weight(copy, grouped, raw, k):
-            copy(
+        def round_weight(grouped, raw, k):
+            nc.scalar.activation(
                 grouped.rearrange("p (t m j) -> p m j t", t=PACK, j=PACK)[:, k * P // 2 : (k + 1) * P // 2, :, :],
                 raw.rearrange("p j (m t) -> p m j t", t=PACK),
+                ACT.Copy, scale=-1.0,
             )
-
-        def halves_of(raw):
-            return [raw[:, :, k * PASS // 2 : (k + 1) * PASS // 2] for k in range(2)]
 
         def mx_tiles(name, pool=held, words_at=None):
             words = pool.tile([P, PASS], U32, name=name + "_words", offset=words_at, align_bytes=64)
@@ -172,71 +176,79 @@ def tile_list_pane_releading_page_kernel(
 
         w2_dealt = [deal_words(b) for b in range(PASSES)]
         fill_plane(tab_s, tab_rows)
+        fill_plane(w2_plane, w2_rows)
+        w2_q = [(w2_dealt[b], deal_scales(b, w2_plane)) for b in range(PASSES)]
         v_scales = held.tile([P, S], U8, align_bytes=64)
         nc.vector.tensor_copy(v_scales[:], tab_s[:].indirect(list1[:]))
         v_words = held.tile([P, S], U32, align_bytes=64)
-        nc.vector.tensor_copy(v_words[:], tab[:].bitcast(U32).indirect(list1[:]))
+        for h in range(2):
+            nc.vector.tensor_copy(v_words[:, half_cols(h)], tab[:].bitcast(U32).indirect(half_list(list1, h)))
         v_q = [(v_words[:, half_cols(h)], v_scales[:, half_cols(h)]) for h in range(2)]
-        w2_plane = shared.tile([P, H], U8, offset=0, align_bytes=64)
-        nc.vector.memset(w2_plane[:].bitcast(I32), 0)
-        fill_plane(w2_plane, w2_rows)
-        w2_q = [(w2_dealt[b], deal_scales(b, w2_plane)) for b in range(PASSES)]
         w1_grouped = rooms[:, 0:2, :].rearrange("p r c -> p (r c)").bitcast(BF16)
-        w1_halves = halves_of(w1_raw0)
         for k in range(2):
-            round_weight(nc.scalar.copy, w1_grouped, w1_halves[k], k)
-        w3_grouped = shared.tile([P, PACK * PASS], BF16, offset=H, align_bytes=64)
-        round_weight(nc.scalar.copy, w3_grouped[:], w3_head[0][:], 0)
-        round_weight(nc.vector.tensor_copy, w3_grouped[:], w3_head[1][:], 1)
-        w1_q = [mx_tiles("w1_0", shared, H + 2 * PACK * PASS), mx_tiles("w1_1")]
-        w3_q = [mx_tiles("w3_0"), mx_tiles("w3_1")]
+            round_weight(w1_grouped, w1_head[k][:], k)
+        w3_grouped = larger_all[:, 0:2, :].rearrange("p r c -> p (r c)").bitcast(BF16)
+        round_weight(w3_grouped, w3_head[0], 0)
+        round_weight(w3_grouped, w3_head[1], 1)
+        w1_q = [mx_tiles("w1_0", shared, H), mx_tiles("w1_1")]
+        w3_q = [mx_tiles("w3_0", shared, T), mx_tiles("w3_1")]
         quantise(w1_q[0], 0, PASS, w1_grouped)
         for c0, c1 in ((0, P), (P, 2 * P), (2 * P, PASS)):
             quantise(w3_q[0], c0, c1, w3_grouped[:, PACK * c0 : PACK * c1])
 
-        def first_products(u):
+        def product(bank, u, weights):
             i, h = divmod(u, 2)
             b, t = divmod(i, PACK)
             v_w, v_s = v_q[h]
             cols = slice(t * P, (t + 1) * P)
-            banks = []
-            for tag, (words, scales) in (("second", w2_q[b]), ("first", w1_q[b]), ("third", w3_q[b])):
-                if tag == "first":
-                    bank = psum.tile([P, HALF], F32, name=tag, tag=tag)
-                else:
-                    bank = turn[(u - (3 if tag == "second" else 1)) % TURNS]
-                if tag == "second":
-                    rhs = words[:, 2 * t * P : 2 * (t + 1) * P].bitcast(FP4X4)
-                else:
-                    rhs = words[:, cols].bitcast(FP8X4)
-                if u < UPRIGHT:
-                    nc.tensor.matmul_mx(
-                        out=bank[:], lhsT=rhs, lhsT_scale=scales[:, cols],
-                        rhs=v_w.bitcast(FP8X4), rhs_scale=v_s, start=True, stop=True,
-                    )
-                for jb in range(HALF // P if u >= UPRIGHT else 0):
-                    js = slice(jb * P, (jb + 1) * P)
-                    nc.tensor.matmul_mx(
-                        out=bank[:, js], lhsT=v_w[:, js].bitcast(FP8X4), lhsT_scale=v_s[:, js],
-                        rhs=rhs, rhs_scale=scales[:, cols], start=True, stop=True,
-                    )
-                banks.append(bank)
-            second, first, third = banks
-            second_sb, big, room = seconds[u % 3][:], larger[u % 4][:], rooms[:, room_index(u), :]
-            nc.scalar.copy(second_sb, second[:])
-            nc.vector.tensor_tensor(big, first[:], second_sb, ALU.max)
+            for jb in range(1 if u < UPRIGHT else HALF // P):
+                js = slice(jb * P, (jb + 1) * P)
+                for k, w_q in enumerate(weights):
+                    words, scales = w_q[b]
+                    if w_q is w2_q:
+                        w_w = words[:, 2 * t * P : 2 * (t + 1) * P].bitcast(FP4X4)
+                    else:
+                        w_w = words[:, cols].bitcast(FP8X4)
+                    first, last = k == 0, k == len(weights) - 1
+                    if u < UPRIGHT:
+                        nc.tensor.matmul_mx(
+                            out=bank[:], lhsT=w_w, lhsT_scale=scales[:, cols],
+                            rhs=v_w.bitcast(FP8X4), rhs_scale=v_s, start=first, stop=last,
+                        )
+                    else:
+                        nc.tensor.matmul_mx(
+                            out=bank[:, js], lhsT=v_w[:, js].bitcast(FP8X4), lhsT_scale=v_s[:, js],
+                            rhs=w_w, rhs_scale=scales[:, cols], start=first, stop=last,
+                        )
+
+        def first_products(u):
+            bank_b, bank_c = turn[u % TURNS], extra[u] if u < UPRIGHT else turn[(u + 1) % TURNS]
+            big, room = larger[u % 4], rooms[:, room_index(u), :]
+            if u >= UNITS - 6:
+                product(bank_b, u, [w2_q, w1_q])
+                product(bank_c, u, [w2_q, w3_q])
+                nc.scalar.activation(big, bank_b[:], ACT.Relu, scale=-1.0)
+                nc.scalar.copy(room, bank_c[:])
+                return
+            bank_a = psum.tile([P, HALF], F32)
+            product(bank_b, u, [w2_q])
+            product(bank_a, u, [w1_q])
+            product(bank_c, u, [w3_q])
+            second_sb = seconds_all[:, u % 4, :]
+            nc.scalar.copy(second_sb, bank_b[:])
+            nc.vector.scalar_tensor_tensor(big, bank_a[:], -1.0, second_sb, ALU.mult, ALU.max)
             if u < UPRIGHT:
-                nc.vector.tensor_tensor(room, big, third[:], ALU.subtract)
+                nc.vector.tensor_tensor(room, big, bank_c[:], ALU.add)
             else:
-                nc.scalar.activation(room, third[:], ACT.Copy, scale=-1.0)
+                nc.scalar.copy(room, bank_c[:])
 
         def new_state(u):
             room = rooms[:, room_index(u), :]
             if u < UPRIGHT:
                 diff = room
             else:
-                diff = turn[u % TURNS][:]
-                blocks = [(src, jb) for src in (larger[u % 4][:], room) for jb in range(HALF // P)]
+                diff = turn[(u + 2) % TURNS][:]
+                blocks = [(src, jb) for src in (larger[u % 4], room) for jb in range(HALF // P)]
                 for k, (src, jb) in enumerate(blocks):
                     js = slice(jb * P, (jb + 1) * P)
                     nc.tensor.matmul(
@@ -246,13 +258,19 @@ def tile_list_pane_releading_page_kernel(
 
         def apply_gain(u):
             b, t = divmod(u // 2, PACK)
-            nc.scalar.activation(state[u % 3][:], side[u % 3][:], ACT.Copy, scale=gain_sb[:, b, t : t + 1])
+            if u < UPRIGHT:
+                rows = wgs_sb[t][:, half_cols(u % 2)]
+                nc.vector.tensor_scalar(larger[(u + 3) % 4], rows, gain_sb[:, b, t : t + 1], None, ALU.mult)
+            else:
+                nc.scalar.activation(state[u % 3][:], side[u % 3][:], ACT.Copy, scale=gain_sb[:, b, t : t + 1])
 
         def put(u):
             i, h = divmod(u, 2)
-            nc.vector.tensor_tensor(
-                pages[i][:].indirect(half_list(list2, h)), state[u % 3][:], wgs_sb[i % PACK][:, half_cols(h)], ALU.mult
-            )
+            if u < UPRIGHT:
+                values, factor = side[u % 3][:], larger[(u + 3) % 4]
+            else:
+                values, factor = state[u % 3][:], wgs_sb[i % PACK][:, half_cols(h)]
+            nc.vector.tensor_tensor(pages[i][:].indirect(half_list(list2, h)), values, factor, ALU.mult)
 
         def fetch(dst, i, h):
             nc.vector.tensor_copy(dst, pages[i][:].indirect(half_list(list3, h)))
@@ -272,9 +290,10 @@ def tile_list_pane_releading_page_kernel(
         later = {}
 
         def weight_piece(room, raw, target, k):
-            nc.scalar.copy(
+            nc.scalar.activation(
                 room.rearrange("p (t m j) -> p m j t", t=2, j=PACK),
                 raw[:].rearrange("p j (m t) -> p m j t", t=PACK)[:, :, :, 2 * k : 2 * k + 2],
+                ACT.Copy, scale=-1.0,
             )
             quantise(target, 2 * k * P, 2 * (k + 1) * P, room)
 
@@ -286,12 +305,12 @@ def tile_list_pane_releading_page_kernel(
             quantise(w4_q[b], n0, n1, room)
 
         def side_job(u, room):
-            if 1 <= u <= 4:
-                k, which = divmod(u - 1, 2)
+            if J0 <= u < J0 + 4:
+                k, which = divmod(u - J0, 2)
                 weight_piece(room, later[("w1", "w3")[which]], (w1_q, w3_q)[which][1], k)
-            elif u in (5, 6):
-                w4_piece(room, u - 5, 0, 2 * P)
-            elif u == 7:
+            elif u in (J0 + 4, J0 + 5):
+                w4_piece(room, u - J0 - 4, 0, 2 * P)
+            elif u == J0 + 6:
                 for b in range(PASSES):
                     w4_piece(room[:, b * PASS : (b + 1) * PASS], b, 2 * P, N)
             elif 11 <= u <= 14:
@@ -300,58 +319,66 @@ def tile_list_pane_releading_page_kernel(
                 interleave(room, planes_of(0, h), c0, c1)
                 quantise(x_q[0, h], c0, c1, room)
 
-        def prepare(u):
-            if u == 0:
-                later["w1"] = load_weight(w1, PASS)
-                later["w3"] = load_weight(w3, PASS)
-                wgs_sb.extend(load_wgs(2, PACK))
-                for i in (2, 3, 4, 5):
-                    pages[i] = load_page(i)
-            if u in (4, 6):
-                pages[6 + (u - 4) // 2] = load_page(6 + (u - 4) // 2)
-            if u in (3, 4):
-                b = u - 3
-                raw = ring.tile([P, PACK, N], F32, name="w4_raw", tag="wide", bufs=3, align_bytes=64)
+        def load_for(u):
+            if u % 2 == 0:
+                if u // 2 < PACK:
+                    wgs_sb.extend(load_wgs(u // 2, u // 2 + 1))
+                pages[u // 2] = load_page(u // 2)
+            if u in (J0 - WL, J0 + 1 - WL):
+                later[("w1", "w3")[u - J0 + WL]] = load_weight((w1, w3)[u - J0 + WL], PASS)
+            if u in (J0 + 4, J0 + 5):
+                b = u - J0 - 4
+                raw = shared.tile([P, PACK, N], F32, name="w4_raw", offset=T + 4 * PASS + 4 * PACK * N * b, align_bytes=64)
                 nc.sync.dma_start(raw[:], w4[b * PASS : (b + 1) * PASS, :].rearrange("(p j) n -> p j n", j=PACK))
                 later["w4", b] = raw
-            if u == 8:
-                later["list4"] = load_list(offs4, "list4")
-                cap_sb = held.tile([P, N // P, PICK], F32)
-                nc.sync.dma_start(cap_sb[:], cap.rearrange("(a p) j -> p a j", p=P))
-                later["cap"] = cap_sb
-                wgo_sb = held.tile([P, PICK], F32)
-                nc.sync.dma_start(wgo_sb[:], wgo)
-                later["wgo"] = wgo_sb
-                for a in range(N // P):
-                    sheet = ring.tile([P, T2], F32, name="sheet", tag="wide", bufs=3, align_bytes=64)
-                    nc.sync.dma_start(sheet[:], page1[a * P : (a + 1) * P, :])
-                    later["sheet", a] = sheet
+
+        def load_last():
+            later["list4"] = load_list(offs4, "list4")
+            cap_sb = held.tile([P, N // P, PICK], F32)
+            nc.sync.dma_start(cap_sb[:], cap.rearrange("(a p) j -> p a j", p=P))
+            later["cap"] = cap_sb
+            wgo_sb = held.tile([P, PICK], F32)
+            nc.sync.dma_start(wgo_sb[:], wgo)
+            later["wgo"] = wgo_sb
+            for a in range(N // P):
+                sheet = ring.tile([P, T2], F32, name="sheet", tag="wide", bufs=3, align_bytes=64)
+                nc.sync.dma_start(sheet[:], page1[a * P : (a + 1) * P, :])
+                later["sheet", a] = sheet
 
         def fetched_at(u):
             i, h = divmod(u - FETCH_LAG, 2)
             return 0 <= i and (i < PACK or h == 0)
 
+        for u in range(1, AHEAD):
+            load_for(u)
         first_products(0)
+        first_products(1)
         for u in range(UNITS + 1):
-            if u + 1 < UNITS:
-                first_products(u + 1)
-            if u < UNITS:
+            if u < UPRIGHT:
+                new_state(u)
+                apply_gain(u)
+            if u + 2 < UNITS:
+                first_products(u + 2)
+            if UPRIGHT <= u < UNITS:
                 new_state(u)
                 apply_gain(u)
             if fetched_at(u - 1):
                 f = u - 1 - FETCH_LAG
-                add_lead(plane_of(f), side[(u - 1) % 3][:], f // 2)
+                add_lead(plane_of(f), larger[(u - 1) % 4], f // 2)
             if u < UNITS:
                 if fetched_at(u):
-                    fetch(side[u % 3][:], *divmod(u - FETCH_LAG, 2))
+                    fetch(larger[u % 4], *divmod(u - FETCH_LAG, 2))
                 put(u)
-                side_job(u, larger[u % 4][:].bitcast(BF16))
-                prepare(u)
+                side_job(u, side[u % 3][:].bitcast(BF16))
+                if u + AHEAD < UNITS:
+                    load_for(u + AHEAD)
+                if u + AHEAD == UNITS:
+                    load_last()
 
         last = UNITS - 1
         spare = [rooms[:, 2 * k : 2 * k + 2, :].rearrange("p r c -> p (r c)") for k in range(3)]
         tile_c, tile_a, tile_b = spare
-        picked_last = side[(last + 1) % 3][:]
+        picked_last = larger[0]
         planes = planes_of(1, 0)
         fetch(picked_last, TILES - 1, 0)
         add_lead(planes[:, PACK - 1, :], picked_last, TILES - 1)
@@ -369,7 +396,7 @@ def tile_list_pane_releading_page_kernel(
         interleave(grouped_b, planes, 0, HALF)
 
         def last_product(a, h):
-            bank = turn[h * (N // P) + a]
+            bank = (turn, extra)[h][a]
             for b in range(PASSES):
                 cols = slice(a * P, (a + 1) * P)
                 w4_words, w4_scales = w4_q[b]
@@ -400,7 +427,7 @@ def tile_list_pane_releading_page_kernel(
         low = tile_a[:, low_half]
         cap_it(low, banks[2], 2, 0)
         place(low, 2, 0)
-        lows = [tile_b[:, low_half], tile_b[:, high_half], larger[0][:]]
+        lows = [tile_b[:, low_half], tile_b[:, high_half], larger[1]]
         banks = [last_product(a, 1) for a in range(N // P)]
         for a in range(N // P):
             cap_it(lows[a], banks[a], a, 1)

@@ -29,8 +29,8 @@ FETCH_LAG = 3
 PLANE_LAG = FETCH_LAG + 1
 ROOMS = UNITS - 1
 TURNS = 3
-J0 = 3
-WL = 1
+J0 = 2
+WL = 0
 AHEAD = 8
 UPRIGHT = 2
 
@@ -224,7 +224,7 @@ def tile_list_pane_releading_page_kernel(
         def first_products(u):
             bank_b, bank_c = turn[u % TURNS], extra[u] if u < UPRIGHT else turn[(u + 1) % TURNS]
             big, room = larger[u % 4], rooms[:, room_index(u), :]
-            if u >= UNITS - 6:
+            if 9 <= u <= 14:
                 product(bank_b, u, [w2_q, w1_q])
                 product(bank_c, u, [w2_q, w3_q])
                 nc.scalar.activation(big, bank_b[:], ACT.Relu, scale=-1.0)
@@ -313,8 +313,8 @@ def tile_list_pane_releading_page_kernel(
             elif u == J0 + 6:
                 for b in range(PASSES):
                     w4_piece(room[:, b * PASS : (b + 1) * PASS], b, 2 * P, N)
-            elif 11 <= u <= 14:
-                h, k = divmod(u - 11, 2)
+            elif 10 <= u <= 13:
+                h, k = divmod(u - 10, 2)
                 c0, c1 = k * HALF // 2, (k + 1) * HALF // 2
                 interleave(room, planes_of(0, h), c0, c1)
                 quantise(x_q[0, h], c0, c1, room)

@@ -20,19 +20,28 @@ ACT = mybir.ActivationFunctionType
 P = 128
 PACK = 4
 PASS = P * PACK
+QUADS = 4
 HALF = 512
 HALF_COLS = HALF // 16
 PASSES = H // PASS
 TILES = H // P
 UNITS = 2 * TILES
+SHEETS = N // P
+
+UPRIGHT = 2
+RELU_UNITS = range(9, 15)
+LOOK_AHEAD = 2
 FETCH_LAG = 3
 PLANE_LAG = FETCH_LAG + 1
-ROOMS = UNITS - 1
+LOAD_AHEAD = 8
+WEIGHT_JOBS = 2
+X_JOBS = 10
+PAGE_SLOTS = 6
+WIDE_SLOTS = SHEETS
 TURNS = 3
-J0 = 2
-WL = 0
-AHEAD = 8
-UPRIGHT = 2
+LARGER = 4
+SIDES = 3
+ROOMS = UNITS - 1
 
 
 def tile_list_pane_releading_page_kernel(
@@ -45,7 +54,7 @@ def tile_list_pane_releading_page_kernel(
         ring = ctx.enter_context(tc.tile_pool(name="ring", bufs=2))
         shared = ctx.enter_context(tc.tile_pool(name="shared", bufs=1))
         psum = ctx.enter_context(tc.psum_pool(name="psum", bufs=2))
-        turns = ctx.enter_context(tc.psum_pool(name="turns", bufs=1))
+        fixed_banks = ctx.enter_context(tc.psum_pool(name="fixed_banks", bufs=1))
 
         def half_list(lst, h):
             return lst[:, h * HALF_COLS : (h + 1) * HALF_COLS]
@@ -60,24 +69,21 @@ def tile_list_pane_releading_page_kernel(
 
         def load_scale_rows(src, width, name):
             rows = held.tile([P, width // 4], I32, name=name)
-            for q in range(4):
+            for q in range(QUADS):
                 nc.sync.dma_start(rows[32 * q : 32 * q + 4, :], src[0, 4 * q : 4 * q + 4, :].bitcast(I32))
             return rows
 
         def fill_plane(plane, rows):
-            for q in range(4):
+            for q in range(QUADS):
                 nc.vector.tensor_copy(plane[32 * q : 32 * q + 4, :].bitcast(I32), rows[32 * q : 32 * q + 4, :])
 
-        def load_weight(w, c0, width=PASS, pool=ring, tag="wide", bufs=3):
-            raw = pool.tile([P, PACK, width], F32, name="raw", tag=tag, bufs=bufs, align_bytes=64)
-            nc.sync.dma_start(raw[:], w[:, c0 : c0 + width].rearrange("(p j) c -> p j c", j=PACK))
-            return raw
+        def by_word(rows):
+            return rows.rearrange("(p j) c -> p j c", j=PACK)
 
         def load_page(i):
             b, t = divmod(i, PACK)
-            page = ring.tile([P, T2], F32, name="page", bufs=6)
-            rows = page0[b * PASS : (b + 1) * PASS, :].rearrange("(p t) m -> p t m", t=PACK)
-            nc.sync.dma_start(page[:], rows[:, t, :])
+            page = ring.tile([P, T2], F32, name="page", bufs=PAGE_SLOTS)
+            nc.sync.dma_start(page[:], by_word(page0[b * PASS : (b + 1) * PASS, :])[:, t, :])
             return page
 
         def load_by_row(src, name):
@@ -85,80 +91,78 @@ def tile_list_pane_releading_page_kernel(
             nc.sync.dma_start(values[:], src.rearrange("(b p t) -> p b t", b=PASSES, t=PACK))
             return values
 
-        def load_wgs(t0, t1):
-            rows = held.tile([P, t1 - t0, S], F32, name="wgs%d" % t0)
-            for q in range(4):
-                nc.sync.dma_start(
-                    rows[32 * q : 32 * q + 32, :, :], wgs.rearrange("(p t) j -> p t j", t=PACK)[:, t0:t1, :]
-                )
-            return [rows[:, t, :] for t in range(t1 - t0)]
+        def load_wgs(t):
+            rows = held.tile([P, 1, S], F32, name="wgs%d" % t)
+            for q in range(QUADS):
+                nc.sync.dma_start(rows[32 * q : 32 * q + 32, :, :], by_word(wgs)[:, t : t + 1, :])
+            return rows[:, 0, :]
 
         ident = held.tile([P, P], F32)
         make_identity(nc, ident[:])
-        tab_s = shared.tile([P, T], U8, offset=0, align_bytes=64)
-        nc.vector.memset(tab_s[:].bitcast(I32), 0)
+        tab_plane = shared.tile([P, T], U8, offset=0, align_bytes=64)
+        nc.vector.memset(tab_plane[:].bitcast(I32), 0)
         w2_plane = held.tile([P, H], U8, align_bytes=64)
         nc.vector.memset(w2_plane[:].bitcast(I32), 0)
-        warm_in = held.tile([P, 1], F32)
-        warm_out = held.tile([P, 1], F32)
-        nc.vector.memset(warm_in[:], 0.0)
-        nc.scalar.activation(warm_out[:], warm_in[:], ACT.Tanh)
 
+        tab_rows = load_scale_rows(tab_scales, T, "tab_rows")
         list1 = load_list(offs, "list1")
         w2_raw = held.tile([P, 2 * H], U8, align_bytes=64)
         nc.sync.dma_start(w2_raw[:].bitcast(I32), w2_words[0].bitcast(I32))
-        tab_rows = load_scale_rows(tab_scales, T, "tab_rows")
-        w1_head = [load_weight(w1, k * PASS // 2, PASS // 2, held, "w1_head%d" % k, 1) for k in range(2)]
+        w1_head = []
+        for k in range(2):
+            raw = held.tile([P, PACK, PASS // 2], F32, name="w1_head%d" % k, align_bytes=64)
+            nc.sync.dma_start(raw[:], by_word(w1[:, k * PASS // 2 : (k + 1) * PASS // 2]))
+            w1_head.append(raw)
         w2_rows = load_scale_rows(w2_scales, H, "w2_rows")
         tab = shared.tile([P, T], I32, offset=T, align_bytes=64)
         nc.sync.dma_start(tab[:], tab_words[0].rearrange("p t i -> p (t i)").bitcast(I32))
-        seconds_all = held.tile([P, 4, HALF], F32)
-        nc.sync.dma_start(seconds_all[:], w3[:, 0:PASS].rearrange("(p j) c -> p j c", j=PACK))
-        w3_head = [seconds_all[:, :, k * PASS // 2 : (k + 1) * PASS // 2] for k in range(2)]
+        seconds = held.tile([P, PACK, HALF], F32)
+        nc.sync.dma_start(seconds[:], by_word(w3[:, 0:PASS]))
         list2 = load_list(offs2, "list2")
         gain_sb = load_by_row(gain, "gain_sb")
         pages = {0: load_page(0)}
-        wgs_sb = load_wgs(0, 1)
+        wgs_sb = [load_wgs(0)]
         lead_sb = load_by_row(lead, "lead_sb")
         list3 = load_list(offs3, "list3")
 
-        larger_all = held.tile([P, 4, HALF], F32, align_bytes=64)
-        larger = [larger_all[:, k, :] for k in range(4)]
-        side = [held.tile([P, HALF], F32, name="side%d" % k, align_bytes=64) for k in range(3)]
-        state = [held.tile([P, HALF], F32, name="state%d" % k) for k in range(3)]
+        larger_ring = held.tile([P, LARGER, HALF], F32, align_bytes=64)
+        larger = [larger_ring[:, k, :] for k in range(LARGER)]
+        side = [held.tile([P, HALF], F32, name="side%d" % k, align_bytes=64) for k in range(SIDES)]
+        state = [held.tile([P, HALF], F32, name="state%d" % k) for k in range(SIDES)]
         rooms = held.tile([P, ROOMS, HALF], F32, align_bytes=64)
-        turn = [turns.tile([P, HALF], F32, name="turn%d" % k) for k in range(TURNS)]
-        extra = [turns.tile([P, HALF], F32, name="extra%d" % k) for k in range(N // P)]
+        turn = [fixed_banks.tile([P, HALF], F32, name="turn%d" % k) for k in range(TURNS)]
+        extra = [fixed_banks.tile([P, HALF], F32, name="extra%d" % k) for k in range(SHEETS)]
 
-        def room_index(u):
-            return (u - PLANE_LAG) % ROOMS
+        def room_of(u):
+            return rooms[:, (u - PLANE_LAG) % ROOMS, :]
 
         def plane_of(f):
-            return rooms[:].bitcast(BF16)[:, room_index(f + PLANE_LAG), 0:HALF]
+            return rooms[:].bitcast(BF16)[:, f, 0:HALF]
 
         def planes_of(b, h):
-            first = room_index(2 * PACK * b + h + PLANE_LAG)
+            first = 2 * PACK * b + h
             return rooms[:].bitcast(BF16)[:, first : first + 2 * PACK - 1 : 2, 0:HALF]
 
-        low_half, high_half = half_cols(0), half_cols(1)
+        def room_pair(k):
+            return rooms[:, 2 * k : 2 * k + 2, :].rearrange("p r c -> p (r c)")
 
         def deal_words(b):
             words = held.tile([P, 2 * PASS], U8, name="w2_words%d" % b, align_bytes=64)
             nc.vector.tensor_copy(
-                words[:].rearrange("p (t m e) -> p m t e", t=PACK, e=2),
-                w2_raw[:, 2 * b * PASS : 2 * (b + 1) * PASS].rearrange("p (m t e) -> p m t e", t=PACK, e=2),
+                words[:].rearrange("p (t m e) -> p t m e", t=PACK, e=2),
+                w2_raw[:, 2 * b * PASS : 2 * (b + 1) * PASS].rearrange("p (m t e) -> p t m e", t=PACK, e=2),
             )
             return words
 
-        def deal_scales(b, plane):
+        def deal_scales(b):
             scales = held.tile([P, PASS], U8, name="w2_scales%d" % b, align_bytes=64)
             nc.vector.tensor_copy(
-                scales[:].rearrange("p (t m) -> p m t", t=PACK),
-                plane[:, b * PASS : (b + 1) * PASS].rearrange("p (m t) -> p m t", t=PACK),
+                scales[:].rearrange("p (t m) -> p t m", t=PACK),
+                w2_plane[:, b * PASS : (b + 1) * PASS].rearrange("p (m t) -> p t m", t=PACK),
             )
             return scales
 
-        def round_weight(grouped, raw, k):
+        def round_negated(grouped, raw, k):
             nc.scalar.activation(
                 grouped.rearrange("p (t m j) -> p m j t", t=PACK, j=PACK)[:, k * P // 2 : (k + 1) * P // 2, :, :],
                 raw.rearrange("p j (m t) -> p m j t", t=PACK),
@@ -174,22 +178,21 @@ def tile_list_pane_releading_page_kernel(
             words, scales = target
             nc.vector.quantize_mx(out=words[:, c0:c1].bitcast(FP8X4), scales=scales[:, c0:c1], in_=grouped)
 
+        fill_plane(tab_plane, tab_rows)
         w2_dealt = [deal_words(b) for b in range(PASSES)]
-        fill_plane(tab_s, tab_rows)
         fill_plane(w2_plane, w2_rows)
-        w2_q = [(w2_dealt[b], deal_scales(b, w2_plane)) for b in range(PASSES)]
+        w2_q = [(w2_dealt[b], deal_scales(b)) for b in range(PASSES)]
         v_scales = held.tile([P, S], U8, align_bytes=64)
-        nc.vector.tensor_copy(v_scales[:], tab_s[:].indirect(list1[:]))
+        nc.vector.tensor_copy(v_scales[:], tab_plane[:].indirect(list1[:]))
         v_words = held.tile([P, S], U32, align_bytes=64)
         for h in range(2):
             nc.vector.tensor_copy(v_words[:, half_cols(h)], tab[:].bitcast(U32).indirect(half_list(list1, h)))
-        v_q = [(v_words[:, half_cols(h)], v_scales[:, half_cols(h)]) for h in range(2)]
-        w1_grouped = rooms[:, 0:2, :].rearrange("p r c -> p (r c)").bitcast(BF16)
+        w1_grouped = room_pair(0).bitcast(BF16)
         for k in range(2):
-            round_weight(w1_grouped, w1_head[k][:], k)
-        w3_grouped = larger_all[:, 0:2, :].rearrange("p r c -> p (r c)").bitcast(BF16)
-        round_weight(w3_grouped, w3_head[0], 0)
-        round_weight(w3_grouped, w3_head[1], 1)
+            round_negated(w1_grouped, w1_head[k][:], k)
+        w3_grouped = larger_ring[:, 0:2, :].rearrange("p r c -> p (r c)").bitcast(BF16)
+        for k in range(2):
+            round_negated(w3_grouped, seconds[:, :, k * PASS // 2 : (k + 1) * PASS // 2], k)
         w1_q = [mx_tiles("w1_0", shared, H), mx_tiles("w1_1")]
         w3_q = [mx_tiles("w3_0", shared, T), mx_tiles("w3_1")]
         quantise(w1_q[0], 0, PASS, w1_grouped)
@@ -199,7 +202,7 @@ def tile_list_pane_releading_page_kernel(
         def product(bank, u, weights):
             i, h = divmod(u, 2)
             b, t = divmod(i, PACK)
-            v_w, v_s = v_q[h]
+            v_w, v_s = v_words[:, half_cols(h)], v_scales[:, half_cols(h)]
             cols = slice(t * P, (t + 1) * P)
             for jb in range(1 if u < UPRIGHT else HALF // P):
                 js = slice(jb * P, (jb + 1) * P)
@@ -223,53 +226,55 @@ def tile_list_pane_releading_page_kernel(
 
         def first_products(u):
             bank_b, bank_c = turn[u % TURNS], extra[u] if u < UPRIGHT else turn[(u + 1) % TURNS]
-            big, room = larger[u % 4], rooms[:, room_index(u), :]
-            if 9 <= u <= 14:
+            summand_1, summand_2 = larger[u % LARGER], room_of(u)
+            if u in RELU_UNITS:
                 product(bank_b, u, [w2_q, w1_q])
                 product(bank_c, u, [w2_q, w3_q])
-                nc.scalar.activation(big, bank_b[:], ACT.Relu, scale=-1.0)
-                nc.scalar.copy(room, bank_c[:])
+                nc.scalar.activation(summand_1, bank_b[:], ACT.Relu, scale=-1.0)
+                nc.scalar.copy(summand_2, bank_c[:])
                 return
             bank_a = psum.tile([P, HALF], F32)
             product(bank_b, u, [w2_q])
             product(bank_a, u, [w1_q])
             product(bank_c, u, [w3_q])
-            second_sb = seconds_all[:, u % 4, :]
+            second_sb = seconds[:, u % PACK, :]
             nc.scalar.copy(second_sb, bank_b[:])
-            nc.vector.scalar_tensor_tensor(big, bank_a[:], -1.0, second_sb, ALU.mult, ALU.max)
+            nc.vector.scalar_tensor_tensor(summand_1, bank_a[:], -1.0, second_sb, ALU.mult, ALU.max)
             if u < UPRIGHT:
-                nc.vector.tensor_tensor(room, big, bank_c[:], ALU.add)
+                nc.vector.tensor_tensor(summand_2, summand_1, bank_c[:], ALU.add)
             else:
-                nc.scalar.copy(room, bank_c[:])
+                nc.scalar.copy(summand_2, bank_c[:])
 
-        def new_state(u):
-            room = rooms[:, room_index(u), :]
+        def take_tanh(u):
             if u < UPRIGHT:
-                diff = room
+                diff = room_of(u)
             else:
-                diff = turn[(u + 2) % TURNS][:]
-                blocks = [(src, jb) for src in (larger[u % 4], room) for jb in range(HALF // P)]
+                diff = turn[(u + LOOK_AHEAD) % TURNS][:]
+                blocks = [(src, jb) for src in (larger[u % LARGER], room_of(u)) for jb in range(HALF // P)]
                 for k, (src, jb) in enumerate(blocks):
                     js = slice(jb * P, (jb + 1) * P)
                     nc.tensor.matmul(
                         diff[:, js], src[:, js], ident[:], start=(k == 0), stop=(k == len(blocks) - 1), is_transpose=True
                     )
-            nc.scalar.activation(side[u % 3][:], diff, ACT.Tanh)
+            nc.scalar.activation(side[u % SIDES][:], diff, ACT.Tanh)
+
+        def gained_wgs(u):
+            return larger[(u + LARGER - 1) % LARGER]
 
         def apply_gain(u):
             b, t = divmod(u // 2, PACK)
+            gain_col = gain_sb[:, b, t : t + 1]
             if u < UPRIGHT:
-                rows = wgs_sb[t][:, half_cols(u % 2)]
-                nc.vector.tensor_scalar(larger[(u + 3) % 4], rows, gain_sb[:, b, t : t + 1], None, ALU.mult)
+                nc.vector.tensor_scalar(gained_wgs(u), wgs_sb[t][:, half_cols(u % 2)], gain_col, None, ALU.mult)
             else:
-                nc.scalar.activation(state[u % 3][:], side[u % 3][:], ACT.Copy, scale=gain_sb[:, b, t : t + 1])
+                nc.scalar.activation(state[u % SIDES][:], side[u % SIDES][:], ACT.Copy, scale=gain_col)
 
         def put(u):
             i, h = divmod(u, 2)
             if u < UPRIGHT:
-                values, factor = side[u % 3][:], larger[(u + 3) % 4]
+                values, factor = side[u % SIDES][:], gained_wgs(u)
             else:
-                values, factor = state[u % 3][:], wgs_sb[i % PACK][:, half_cols(h)]
+                values, factor = state[u % SIDES][:], wgs_sb[i % PACK][:, half_cols(h)]
             nc.vector.tensor_tensor(pages[i][:].indirect(half_list(list2, h)), values, factor, ALU.mult)
 
         def fetch(dst, i, h):
@@ -279,126 +284,122 @@ def tile_list_pane_releading_page_kernel(
             b, t = divmod(i, PACK)
             nc.scalar.activation(dst, picked, ACT.Identity, bias=lead_sb[:, b, t : t + 1])
 
-        def interleave(grouped, planes, c0, c1):
+        def interleave(grouped, planes):
             nc.scalar.copy(
                 grouped.rearrange("p (c i t) -> p c t i", i=4, t=PACK),
-                planes[:, :, c0:c1].rearrange("p t (c i) -> p c t i", i=4),
+                planes.rearrange("p t (c i) -> p c t i", i=4),
             )
 
         x_q = {(b, h): mx_tiles("x_%d_%d" % (b, h)) for b in range(PASSES) for h in range(2)}
         w4_q = [mx_tiles("w4_%d" % b) for b in range(PASSES)]
-        later = {}
-
-        def weight_piece(room, raw, target, k):
-            nc.scalar.activation(
-                room.rearrange("p (t m j) -> p m j t", t=2, j=PACK),
-                raw[:].rearrange("p j (m t) -> p m j t", t=PACK)[:, :, :, 2 * k : 2 * k + 2],
-                ACT.Copy, scale=-1.0,
-            )
-            quantise(target, 2 * k * P, 2 * (k + 1) * P, room)
-
-        def w4_piece(room, b, n0, n1):
-            nc.scalar.copy(
-                room.rearrange("p (c i t) -> p c t i", i=4, t=PACK),
-                later["w4", b][:, :, n0:n1].rearrange("p t (c i) -> p c t i", i=4),
-            )
-            quantise(w4_q[b], n0, n1, room)
+        late_raw = []
+        w4_raw = []
 
         def side_job(u, room):
-            if J0 <= u < J0 + 4:
-                k, which = divmod(u - J0, 2)
-                weight_piece(room, later[("w1", "w3")[which]], (w1_q, w3_q)[which][1], k)
-            elif u in (J0 + 4, J0 + 5):
-                w4_piece(room, u - J0 - 4, 0, 2 * P)
-            elif u == J0 + 6:
+            job = u - WEIGHT_JOBS
+            if 0 <= job < 4:
+                k, which = divmod(job, 2)
+                nc.scalar.activation(
+                    room.rearrange("p (t m j) -> p m j t", t=2, j=PACK),
+                    late_raw[which][:].rearrange("p j (m t) -> p m j t", t=PACK)[:, :, :, 2 * k : 2 * k + 2],
+                    ACT.Copy, scale=-1.0,
+                )
+                quantise((w1_q, w3_q)[which][1], 2 * k * P, 2 * (k + 1) * P, room)
+            elif job in (4, 5):
+                interleave(room, w4_raw[job - 4][:, :, 0 : 2 * P])
+                quantise(w4_q[job - 4], 0, 2 * P, room)
+            elif job == 6:
                 for b in range(PASSES):
-                    w4_piece(room[:, b * PASS : (b + 1) * PASS], b, 2 * P, N)
-            elif 10 <= u <= 13:
-                h, k = divmod(u - 10, 2)
+                    part = room[:, b * PASS : (b + 1) * PASS]
+                    interleave(part, w4_raw[b][:, :, 2 * P : N])
+                    quantise(w4_q[b], 2 * P, N, part)
+            elif X_JOBS <= u < X_JOBS + 4:
+                h, k = divmod(u - X_JOBS, 2)
                 c0, c1 = k * HALF // 2, (k + 1) * HALF // 2
-                interleave(room, planes_of(0, h), c0, c1)
+                interleave(room, planes_of(0, h)[:, :, c0:c1])
                 quantise(x_q[0, h], c0, c1, room)
 
         def load_for(u):
+            job = u - WEIGHT_JOBS
             if u % 2 == 0:
                 if u // 2 < PACK:
-                    wgs_sb.extend(load_wgs(u // 2, u // 2 + 1))
+                    wgs_sb.append(load_wgs(u // 2))
                 pages[u // 2] = load_page(u // 2)
-            if u in (J0 - WL, J0 + 1 - WL):
-                later[("w1", "w3")[u - J0 + WL]] = load_weight((w1, w3)[u - J0 + WL], PASS)
-            if u in (J0 + 4, J0 + 5):
-                b = u - J0 - 4
-                raw = shared.tile([P, PACK, N], F32, name="w4_raw", offset=T + 4 * PASS + 4 * PACK * N * b, align_bytes=64)
-                nc.sync.dma_start(raw[:], w4[b * PASS : (b + 1) * PASS, :].rearrange("(p j) n -> p j n", j=PACK))
-                later["w4", b] = raw
+            if job in (0, 1):
+                raw = ring.tile([P, PACK, PASS], F32, name="late_raw", tag="wide", bufs=WIDE_SLOTS, align_bytes=64)
+                nc.sync.dma_start(raw[:], by_word((w1, w3)[job][:, PASS : 2 * PASS]))
+                late_raw.append(raw)
+            if job in (4, 5):
+                b = job - 4
+                behind_codes = T + 4 * PASS
+                raw = shared.tile(
+                    [P, PACK, N], F32, name="w4_raw", offset=behind_codes + 4 * PACK * N * b, align_bytes=64
+                )
+                nc.sync.dma_start(raw[:], by_word(w4[b * PASS : (b + 1) * PASS, :]))
+                w4_raw.append(raw)
 
         def load_last():
-            later["list4"] = load_list(offs4, "list4")
-            cap_sb = held.tile([P, N // P, PICK], F32)
+            list4 = load_list(offs4, "list4")
+            cap_sb = held.tile([P, SHEETS, PICK], F32)
             nc.sync.dma_start(cap_sb[:], cap.rearrange("(a p) j -> p a j", p=P))
-            later["cap"] = cap_sb
             wgo_sb = held.tile([P, PICK], F32)
             nc.sync.dma_start(wgo_sb[:], wgo)
-            later["wgo"] = wgo_sb
-            for a in range(N // P):
-                sheet = ring.tile([P, T2], F32, name="sheet", tag="wide", bufs=3, align_bytes=64)
+            sheets = []
+            for a in range(SHEETS):
+                sheet = ring.tile([P, T2], F32, name="sheet", tag="wide", bufs=WIDE_SLOTS, align_bytes=64)
                 nc.sync.dma_start(sheet[:], page1[a * P : (a + 1) * P, :])
-                later["sheet", a] = sheet
+                sheets.append(sheet)
+            return list4, cap_sb, wgo_sb, sheets
 
-        def fetched_at(u):
+        def fetches(u):
             i, h = divmod(u - FETCH_LAG, 2)
             return 0 <= i and (i < PACK or h == 0)
 
-        for u in range(1, AHEAD):
+        for u in range(1, LOAD_AHEAD):
             load_for(u)
-        first_products(0)
-        first_products(1)
+        for u in range(LOOK_AHEAD):
+            first_products(u)
         for u in range(UNITS + 1):
             if u < UPRIGHT:
-                new_state(u)
+                take_tanh(u)
                 apply_gain(u)
-            if u + 2 < UNITS:
-                first_products(u + 2)
+            if u + LOOK_AHEAD < UNITS:
+                first_products(u + LOOK_AHEAD)
             if UPRIGHT <= u < UNITS:
-                new_state(u)
+                take_tanh(u)
                 apply_gain(u)
-            if fetched_at(u - 1):
-                f = u - 1 - FETCH_LAG
-                add_lead(plane_of(f), larger[(u - 1) % 4], f // 2)
+            if fetches(u - 1):
+                f = u - PLANE_LAG
+                add_lead(plane_of(f), larger[(u - 1) % LARGER], f // 2)
             if u < UNITS:
-                if fetched_at(u):
-                    fetch(larger[u % 4], *divmod(u - FETCH_LAG, 2))
+                if fetches(u):
+                    fetch(larger[u % LARGER], *divmod(u - FETCH_LAG, 2))
                 put(u)
-                side_job(u, side[u % 3][:].bitcast(BF16))
-                if u + AHEAD < UNITS:
-                    load_for(u + AHEAD)
-                if u + AHEAD == UNITS:
-                    load_last()
+                side_job(u, side[u % SIDES][:].bitcast(BF16))
+                if u + LOAD_AHEAD < UNITS:
+                    load_for(u + LOAD_AHEAD)
+                if u + LOAD_AHEAD == UNITS:
+                    list4, cap_sb, wgo_sb, sheets = load_last()
 
-        last = UNITS - 1
-        spare = [rooms[:, 2 * k : 2 * k + 2, :].rearrange("p r c -> p (r c)") for k in range(3)]
-        tile_c, tile_a, tile_b = spare
+        first_x, second_x, capped = [room_pair(k) for k in range(3)]
         picked_last = larger[0]
         planes = planes_of(1, 0)
         fetch(picked_last, TILES - 1, 0)
         add_lead(planes[:, PACK - 1, :], picked_last, TILES - 1)
-        grouped_a = tile_c.bitcast(BF16)
-        interleave(grouped_a, planes, 0, HALF)
-        targets = [state[last % 3][:], wgs_sb[PACK - 1][:, high_half], picked_last]
+        interleave(first_x.bitcast(BF16), planes)
+        picked = [state[(UNITS - 1) % SIDES][:], wgs_sb[PACK - 1][:, half_cols(1)], picked_last, first_x[:, half_cols(0)]]
         for t in range(PACK - 1):
-            fetch(targets[t], PACK + t, 1)
-        quantise(x_q[1, 0], 0, PASS, grouped_a)
-        targets.append(tile_c[:, low_half])
-        fetch(targets[-1], TILES - 1, 1)
+            fetch(picked[t], PACK + t, 1)
+        quantise(x_q[1, 0], 0, PASS, first_x.bitcast(BF16))
+        fetch(picked[PACK - 1], TILES - 1, 1)
         for t in range(PACK):
-            add_lead(planes[:, t, :], targets[t], PACK + t)
-        grouped_b = tile_a.bitcast(BF16)
-        interleave(grouped_b, planes, 0, HALF)
+            add_lead(planes[:, t, :], picked[t], PACK + t)
+        interleave(second_x.bitcast(BF16), planes)
 
         def last_product(a, h):
             bank = (turn, extra)[h][a]
+            cols = slice(a * P, (a + 1) * P)
             for b in range(PASSES):
-                cols = slice(a * P, (a + 1) * P)
                 w4_words, w4_scales = w4_q[b]
                 x_words, x_scales = x_q[b, h]
                 nc.tensor.matmul_mx(
@@ -407,29 +408,25 @@ def tile_list_pane_releading_page_kernel(
                 )
             return bank
 
-        def cap_it(low, bank, a, h):
-            nc.vector.tensor_tensor(low, bank[:], later["cap"][:, a, half_cols(h)], ALU.min)
+        def take_min(low, bank, a, h):
+            nc.vector.tensor_tensor(low, bank[:], cap_sb[:, a, half_cols(h)], ALU.min)
 
         def place(low, a, h):
-            sheet = later["sheet", a]
-            nc.vector.tensor_tensor(
-                sheet[:].indirect(half_list(later["list4"], h)), low, later["wgo"][:, half_cols(h)], ALU.mult
-            )
+            nc.vector.tensor_tensor(sheets[a][:].indirect(half_list(list4, h)), low, wgo_sb[:, half_cols(h)], ALU.mult)
             if h == 1:
-                nc.sync.dma_start(out[a * P : (a + 1) * P, :], sheet[:])
+                nc.sync.dma_start(out[a * P : (a + 1) * P, :], sheets[a][:])
 
-        banks = [last_product(a, 0) for a in range(N // P)]
-        for a in range(2):
-            cap_it(tile_b[:, half_cols(a)], banks[a], a, 0)
-        for a in range(2):
-            place(tile_b[:, half_cols(a)], a, 0)
-        quantise(x_q[1, 1], 0, PASS, grouped_b)
-        low = tile_a[:, low_half]
-        cap_it(low, banks[2], 2, 0)
-        place(low, 2, 0)
-        lows = [tile_b[:, low_half], tile_b[:, high_half], larger[1]]
-        banks = [last_product(a, 1) for a in range(N // P)]
-        for a in range(N // P):
-            cap_it(lows[a], banks[a], a, 1)
-        for a in range(N // P):
+        banks = [last_product(a, 0) for a in range(SHEETS)]
+        for a in range(SHEETS - 1):
+            take_min(capped[:, half_cols(a)], banks[a], a, 0)
+        for a in range(SHEETS - 1):
+            place(capped[:, half_cols(a)], a, 0)
+        quantise(x_q[1, 1], 0, PASS, second_x.bitcast(BF16))
+        take_min(second_x[:, half_cols(0)], banks[SHEETS - 1], SHEETS - 1, 0)
+        place(second_x[:, half_cols(0)], SHEETS - 1, 0)
+        lows = [capped[:, half_cols(0)], capped[:, half_cols(1)], larger[1]]
+        banks = [last_product(a, 1) for a in range(SHEETS)]
+        for a in range(SHEETS):
+            take_min(lows[a], banks[a], a, 1)
+        for a in range(SHEETS):
             place(lows[a], a, 1)

from contextlib import ExitStack

import concourse.mybir as mybir
from concourse.masks import make_identity

K, T, S, H, T2, PICK, N = 512, 4096, 1024, 1024, 2048, 1024, 384
FLOPS = 2 * 3 * K * H * S + 2 * H * N * PICK

F32 = mybir.dt.float32
BF16 = mybir.dt.bfloat16
I32 = mybir.dt.int32
U32 = mybir.dt.uint32
U16 = mybir.dt.uint16
U8 = mybir.dt.uint8
FP8X4 = mybir.dt.float8_e4m3fn_x4
FP4X4 = mybir.dt.float4_e2m1fn_x4
ALU = mybir.AluOpType
ACT = mybir.ActivationFunctionType

P = 128
PACK = 4
PASS = P * PACK
QUADS = 4
HALF = 512
HALF_COLS = HALF // 16
PASSES = H // PASS
TILES = H // P
UNITS = 2 * TILES
SHEETS = N // P

UPRIGHT = 2
RELU_UNITS = range(9, 15)
LOOK_AHEAD = 2
FETCH_LAG = 3
PLANE_LAG = FETCH_LAG + 1
LOAD_AHEAD = 8
WEIGHT_JOBS = 2
X_JOBS = 10
PAGE_SLOTS = 6
WIDE_SLOTS = SHEETS
TURNS = 3
LARGER = 4
SIDES = 3
ROOMS = UNITS - 1


def tile_list_pane_releading_page_kernel(
    tc, tab_words, tab_scales, offs, offs2, offs3, offs4, w1, w2_words, w2_scales, w3,
    gain, wgs, page0, lead, w4, cap, wgo, page1, out,
):
    nc = tc.nc
    with ExitStack() as ctx:
        held = ctx.enter_context(tc.tile_pool(name="held", bufs=1))
        ring = ctx.enter_context(tc.tile_pool(name="ring", bufs=2))
        shared = ctx.enter_context(tc.tile_pool(name="shared", bufs=1))
        psum = ctx.enter_context(tc.psum_pool(name="psum", bufs=2))
        fixed_banks = ctx.enter_context(tc.psum_pool(name="fixed_banks", bufs=1))

        def half_list(lst, h):
            return lst[:, h * HALF_COLS : (h + 1) * HALF_COLS]

        def half_cols(h):
            return slice(h * HALF, (h + 1) * HALF)

        def load_list(src, name):
            lst = held.tile([P, S // 16], U16, name=name)
            nc.sync.dma_start(lst[:], src)
            return lst

        def load_scale_rows(src, width, name):
            rows = held.tile([P, width // 4], I32, name=name)
            for q in range(QUADS):
                nc.sync.dma_start(rows[32 * q : 32 * q + 4, :], src[0, 4 * q : 4 * q + 4, :].bitcast(I32))
            return rows

        def fill_plane(plane, rows):
            for q in range(QUADS):
                nc.vector.tensor_copy(plane[32 * q : 32 * q + 4, :].bitcast(I32), rows[32 * q : 32 * q + 4, :])

        def by_word(rows):
            return rows.rearrange("(p j) c -> p j c", j=PACK)

        def load_page(i):
            b, t = divmod(i, PACK)
            page = ring.tile([P, T2], F32, name="page", bufs=PAGE_SLOTS)
            nc.sync.dma_start(page[:], by_word(page0[b * PASS : (b + 1) * PASS, :])[:, t, :])
            return page

        def load_by_row(src, name):
            values = held.tile([P, PASSES, PACK], F32, name=name)
            nc.sync.dma_start(values[:], src.rearrange("(b p t) -> p b t", b=PASSES, t=PACK))
            return values

        def load_wgs(t):
            rows = held.tile([P, 1, S], F32, name="wgs%d" % t)
            for q in range(QUADS):
                nc.sync.dma_start(rows[32 * q : 32 * q + 32, :, :], by_word(wgs)[:, t : t + 1, :])
            return rows[:, 0, :]

        ident = held.tile([P, P], F32)
        make_identity(nc, ident[:])
        tab_plane = shared.tile([P, T], U8, offset=0, align_bytes=64)
        nc.vector.memset(tab_plane[:].bitcast(I32), 0)
        w2_plane = held.tile([P, H], U8, align_bytes=64)
        nc.vector.memset(w2_plane[:].bitcast(I32), 0)

        tab_rows = load_scale_rows(tab_scales, T, "tab_rows")
        list1 = load_list(offs, "list1")
        w2_raw = held.tile([P, 2 * H], U8, align_bytes=64)
        nc.sync.dma_start(w2_raw[:].bitcast(I32), w2_words[0].bitcast(I32))
        w1_head = []
        for k in range(2):
            raw = held.tile([P, PACK, PASS // 2], F32, name="w1_head%d" % k, align_bytes=64)
            nc.sync.dma_start(raw[:], by_word(w1[:, k * PASS // 2 : (k + 1) * PASS // 2]))
            w1_head.append(raw)
        w2_rows = load_scale_rows(w2_scales, H, "w2_rows")
        tab = shared.tile([P, T], I32, offset=T, align_bytes=64)
        nc.sync.dma_start(tab[:], tab_words[0].rearrange("p t i -> p (t i)").bitcast(I32))
        seconds = held.tile([P, PACK, HALF], F32)
        nc.sync.dma_start(seconds[:], by_word(w3[:, 0:PASS]))
        list2 = load_list(offs2, "list2")
        gain_sb = load_by_row(gain, "gain_sb")
        pages = {0: load_page(0)}
        wgs_sb = [load_wgs(0)]
        lead_sb = load_by_row(lead, "lead_sb")
        list3 = load_list(offs3, "list3")

        larger_ring = held.tile([P, LARGER, HALF], F32, align_bytes=64)
        larger = [larger_ring[:, k, :] for k in range(LARGER)]
        side = [held.tile([P, HALF], F32, name="side%d" % k, align_bytes=64) for k in range(SIDES)]
        state = [held.tile([P, HALF], F32, name="state%d" % k) for k in range(SIDES)]
        rooms = held.tile([P, ROOMS, HALF], F32, align_bytes=64)
        turn = [fixed_banks.tile([P, HALF], F32, name="turn%d" % k) for k in range(TURNS)]
        extra = [fixed_banks.tile([P, HALF], F32, name="extra%d" % k) for k in range(SHEETS)]

        def room_of(u):
            return rooms[:, (u - PLANE_LAG) % ROOMS, :]

        def plane_of(f):
            return rooms[:].bitcast(BF16)[:, f, 0:HALF]

        def planes_of(b, h):
            first = 2 * PACK * b + h
            return rooms[:].bitcast(BF16)[:, first : first + 2 * PACK - 1 : 2, 0:HALF]

        def room_pair(k):
            return rooms[:, 2 * k : 2 * k + 2, :].rearrange("p r c -> p (r c)")

        def deal_words(b):
            words = held.tile([P, 2 * PASS], U8, name="w2_words%d" % b, align_bytes=64)
            nc.vector.tensor_copy(
                words[:].rearrange("p (t m e) -> p t m e", t=PACK, e=2),
                w2_raw[:, 2 * b * PASS : 2 * (b + 1) * PASS].rearrange("p (m t e) -> p t m e", t=PACK, e=2),
            )
            return words

        def deal_scales(b):
            scales = held.tile([P, PASS], U8, name="w2_scales%d" % b, align_bytes=64)
            nc.vector.tensor_copy(
                scales[:].rearrange("p (t m) -> p t m", t=PACK),
                w2_plane[:, b * PASS : (b + 1) * PASS].rearrange("p (m t) -> p t m", t=PACK),
            )
            return scales

        def round_negated(grouped, raw, k):
            nc.scalar.activation(
                grouped.rearrange("p (t m j) -> p m j t", t=PACK, j=PACK)[:, k * P // 2 : (k + 1) * P // 2, :, :],
                raw.rearrange("p j (m t) -> p m j t", t=PACK),
                ACT.Copy, scale=-1.0,
            )

        def mx_tiles(name, pool=held, words_at=None):
            words = pool.tile([P, PASS], U32, name=name + "_words", offset=words_at, align_bytes=64)
            scales = held.tile([P, PASS], U8, name=name + "_scales", align_bytes=64)
            return words, scales

        def quantise(target, c0, c1, grouped):
            words, scales = target
            nc.vector.quantize_mx(out=words[:, c0:c1].bitcast(FP8X4), scales=scales[:, c0:c1], in_=grouped)

        fill_plane(tab_plane, tab_rows)
        w2_dealt = [deal_words(b) for b in range(PASSES)]
        fill_plane(w2_plane, w2_rows)
        w2_q = [(w2_dealt[b], deal_scales(b)) for b in range(PASSES)]
        v_scales = held.tile([P, S], U8, align_bytes=64)
        nc.vector.tensor_copy(v_scales[:], tab_plane[:].indirect(list1[:]))
        v_words = held.tile([P, S], U32, align_bytes=64)
        for h in range(2):
            nc.vector.tensor_copy(v_words[:, half_cols(h)], tab[:].bitcast(U32).indirect(half_list(list1, h)))
        w1_grouped = room_pair(0).bitcast(BF16)
        for k in range(2):
            round_negated(w1_grouped, w1_head[k][:], k)
        w3_grouped = larger_ring[:, 0:2, :].rearrange("p r c -> p (r c)").bitcast(BF16)
        for k in range(2):
            round_negated(w3_grouped, seconds[:, :, k * PASS // 2 : (k + 1) * PASS // 2], k)
        w1_q = [mx_tiles("w1_0", shared, H), mx_tiles("w1_1")]
        w3_q = [mx_tiles("w3_0", shared, T), mx_tiles("w3_1")]
        quantise(w1_q[0], 0, PASS, w1_grouped)
        for c0, c1 in ((0, P), (P, 2 * P), (2 * P, PASS)):
            quantise(w3_q[0], c0, c1, w3_grouped[:, PACK * c0 : PACK * c1])

        def product(bank, u, weights):
            i, h = divmod(u, 2)
            b, t = divmod(i, PACK)
            v_w, v_s = v_words[:, half_cols(h)], v_scales[:, half_cols(h)]
            cols = slice(t * P, (t + 1) * P)
            for jb in range(1 if u < UPRIGHT else HALF // P):
                js = slice(jb * P, (jb + 1) * P)
                for k, w_q in enumerate(weights):
                    words, scales = w_q[b]
                    if w_q is w2_q:
                        w_w = words[:, 2 * t * P : 2 * (t + 1) * P].bitcast(FP4X4)
                    else:
                        w_w = words[:, cols].bitcast(FP8X4)
                    first, last = k == 0, k == len(weights) - 1
                    if u < UPRIGHT:
                        nc.tensor.matmul_mx(
                            out=bank[:], lhsT=w_w, lhsT_scale=scales[:, cols],
                            rhs=v_w.bitcast(FP8X4), rhs_scale=v_s, start=first, stop=last,
                        )
                    else:
                        nc.tensor.matmul_mx(
                            out=bank[:, js], lhsT=v_w[:, js].bitcast(FP8X4), lhsT_scale=v_s[:, js],
                            rhs=w_w, rhs_scale=scales[:, cols], start=first, stop=last,
                        )

        def first_products(u):
            bank_b, bank_c = turn[u % TURNS], extra[u] if u < UPRIGHT else turn[(u + 1) % TURNS]
            summand_1, summand_2 = larger[u % LARGER], room_of(u)
            if u in RELU_UNITS:
                product(bank_b, u, [w2_q, w1_q])
                product(bank_c, u, [w2_q, w3_q])
                nc.scalar.activation(summand_1, bank_b[:], ACT.Relu, scale=-1.0)
                nc.scalar.copy(summand_2, bank_c[:])
                return
            bank_a = psum.tile([P, HALF], F32)
            product(bank_b, u, [w2_q])
            product(bank_a, u, [w1_q])
            product(bank_c, u, [w3_q])
            second_sb = seconds[:, u % PACK, :]
            nc.scalar.copy(second_sb, bank_b[:])
            nc.vector.scalar_tensor_tensor(summand_1, bank_a[:], -1.0, second_sb, ALU.mult, ALU.max)
            if u < UPRIGHT:
                nc.vector.tensor_tensor(summand_2, summand_1, bank_c[:], ALU.add)
            else:
                nc.scalar.copy(summand_2, bank_c[:])

        def take_tanh(u):
            if u < UPRIGHT:
                diff = room_of(u)
            else:
                diff = turn[(u + LOOK_AHEAD) % TURNS][:]
                blocks = [(src, jb) for src in (larger[u % LARGER], room_of(u)) for jb in range(HALF // P)]
                for k, (src, jb) in enumerate(blocks):
                    js = slice(jb * P, (jb + 1) * P)
                    nc.tensor.matmul(
                        diff[:, js], src[:, js], ident[:], start=(k == 0), stop=(k == len(blocks) - 1), is_transpose=True
                    )
            nc.scalar.activation(side[u % SIDES][:], diff, ACT.Tanh)

        def gained_wgs(u):
            return larger[(u + LARGER - 1) % LARGER]

        def apply_gain(u):
            b, t = divmod(u // 2, PACK)
            gain_col = gain_sb[:, b, t : t + 1]
            if u < UPRIGHT:
                nc.vector.tensor_scalar(gained_wgs(u), wgs_sb[t][:, half_cols(u % 2)], gain_col, None, ALU.mult)
            else:
                nc.scalar.activation(state[u % SIDES][:], side[u % SIDES][:], ACT.Copy, scale=gain_col)

        def put(u):
            i, h = divmod(u, 2)
            if u < UPRIGHT:
                values, factor = side[u % SIDES][:], gained_wgs(u)
            else:
                values, factor = state[u % SIDES][:], wgs_sb[i % PACK][:, half_cols(h)]
            nc.vector.tensor_tensor(pages[i][:].indirect(half_list(list2, h)), values, factor, ALU.mult)

        def fetch(dst, i, h):
            nc.vector.tensor_copy(dst, pages[i][:].indirect(half_list(list3, h)))

        def add_lead(dst, picked, i):
            b, t = divmod(i, PACK)
            nc.scalar.activation(dst, picked, ACT.Identity, bias=lead_sb[:, b, t : t + 1])

        def interleave(grouped, planes):
            nc.scalar.copy(
                grouped.rearrange("p (c i t) -> p c t i", i=4, t=PACK),
                planes.rearrange("p t (c i) -> p c t i", i=4),
            )

        x_q = {(b, h): mx_tiles("x_%d_%d" % (b, h)) for b in range(PASSES) for h in range(2)}
        w4_q = [mx_tiles("w4_%d" % b) for b in range(PASSES)]
        late_raw = []
        w4_raw = []

        def side_job(u, room):
            job = u - WEIGHT_JOBS
            if 0 <= job < 4:
                k, which = divmod(job, 2)
                nc.scalar.activation(
                    room.rearrange("p (t m j) -> p m j t", t=2, j=PACK),
                    late_raw[which][:].rearrange("p j (m t) -> p m j t", t=PACK)[:, :, :, 2 * k : 2 * k + 2],
                    ACT.Copy, scale=-1.0,
                )
                quantise((w1_q, w3_q)[which][1], 2 * k * P, 2 * (k + 1) * P, room)
            elif job in (4, 5):
                interleave(room, w4_raw[job - 4][:, :, 0 : 2 * P])
                quantise(w4_q[job - 4], 0, 2 * P, room)
            elif job == 6:
                for b in range(PASSES):
                    part = room[:, b * PASS : (b + 1) * PASS]
                    interleave(part, w4_raw[b][:, :, 2 * P : N])
                    quantise(w4_q[b], 2 * P, N, part)
            elif X_JOBS <= u < X_JOBS + 4:
                h, k = divmod(u - X_JOBS, 2)
                c0, c1 = k * HALF // 2, (k + 1) * HALF // 2
                interleave(room, planes_of(0, h)[:, :, c0:c1])
                quantise(x_q[0, h], c0, c1, room)

        def load_for(u):
            job = u - WEIGHT_JOBS
            if u % 2 == 0:
                if u // 2 < PACK:
                    wgs_sb.append(load_wgs(u // 2))
                pages[u // 2] = load_page(u // 2)
            if job in (0, 1):
                raw = ring.tile([P, PACK, PASS], F32, name="late_raw", tag="wide", bufs=WIDE_SLOTS, align_bytes=64)
                nc.sync.dma_start(raw[:], by_word((w1, w3)[job][:, PASS : 2 * PASS]))
                late_raw.append(raw)
            if job in (4, 5):
                b = job - 4
                behind_codes = T + 4 * PASS
                raw = shared.tile(
                    [P, PACK, N], F32, name="w4_raw", offset=behind_codes + 4 * PACK * N * b, align_bytes=64
                )
                nc.sync.dma_start(raw[:], by_word(w4[b * PASS : (b + 1) * PASS, :]))
                w4_raw.append(raw)

        def load_last():
            list4 = load_list(offs4, "list4")
            cap_sb = held.tile([P, SHEETS, PICK], F32)
            nc.sync.dma_start(cap_sb[:], cap.rearrange("(a p) j -> p a j", p=P))
            wgo_sb = held.tile([P, PICK], F32)
            nc.sync.dma_start(wgo_sb[:], wgo)
            sheets = []
            for a in range(SHEETS):
                sheet = ring.tile([P, T2], F32, name="sheet", tag="wide", bufs=WIDE_SLOTS, align_bytes=64)
                nc.sync.dma_start(sheet[:], page1[a * P : (a + 1) * P, :])
                sheets.append(sheet)
            return list4, cap_sb, wgo_sb, sheets

        def fetches(u):
            i, h = divmod(u - FETCH_LAG, 2)
            return 0 <= i and (i < PACK or h == 0)

        for u in range(1, LOAD_AHEAD):
            load_for(u)
        for u in range(LOOK_AHEAD):
            first_products(u)
        for u in range(UNITS + 1):
            if u < UPRIGHT:
                take_tanh(u)
                apply_gain(u)
            if u + LOOK_AHEAD < UNITS:
                first_products(u + LOOK_AHEAD)
            if UPRIGHT <= u < UNITS:
                take_tanh(u)
                apply_gain(u)
            if fetches(u - 1):
                f = u - PLANE_LAG
                add_lead(plane_of(f), larger[(u - 1) % LARGER], f // 2)
            if u < UNITS:
                if fetches(u):
                    fetch(larger[u % LARGER], *divmod(u - FETCH_LAG, 2))
                put(u)
                side_job(u, side[u % SIDES][:].bitcast(BF16))
                if u + LOAD_AHEAD < UNITS:
                    load_for(u + LOAD_AHEAD)
                if u + LOAD_AHEAD == UNITS:
                    list4, cap_sb, wgo_sb, sheets = load_last()

        first_x, second_x, capped = [room_pair(k) for k in range(3)]
        picked_last = larger[0]
        planes = planes_of(1, 0)
        fetch(picked_last, TILES - 1, 0)
        add_lead(planes[:, PACK - 1, :], picked_last, TILES - 1)
        interleave(first_x.bitcast(BF16), planes)
        picked = [state[(UNITS - 1) % SIDES][:], wgs_sb[PACK - 1][:, half_cols(1)], picked_last, first_x[:, half_cols(0)]]
        for t in range(PACK - 1):
            fetch(picked[t], PACK + t, 1)
        quantise(x_q[1, 0], 0, PASS, first_x.bitcast(BF16))
        fetch(picked[PACK - 1], TILES - 1, 1)
        for t in range(PACK):
            add_lead(planes[:, t, :], picked[t], PACK + t)
        interleave(second_x.bitcast(BF16), planes)

        def last_product(a, h):
            bank = (turn, extra)[h][a]
            cols = slice(a * P, (a + 1) * P)
            for b in range(PASSES):
                w4_words, w4_scales = w4_q[b]
                x_words, x_scales = x_q[b, h]
                nc.tensor.matmul_mx(
                    out=bank[:], lhsT=w4_words[:, cols].bitcast(FP8X4), lhsT_scale=w4_scales[:, cols],
                    rhs=x_words[:].bitcast(FP8X4), rhs_scale=x_scales[:], start=(b == 0), stop=(b == PASSES - 1),
                )
            return bank

        def take_min(low, bank, a, h):
            nc.vector.tensor_tensor(low, bank[:], cap_sb[:, a, half_cols(h)], ALU.min)

        def place(low, a, h):
            nc.vector.tensor_tensor(sheets[a][:].indirect(half_list(list4, h)), low, wgo_sb[:, half_cols(h)], ALU.mult)
            if h == 1:
                nc.sync.dma_start(out[a * P : (a + 1) * P, :], sheets[a][:])

        banks = [last_product(a, 0) for a in range(SHEETS)]
        for a in range(SHEETS - 1):
            take_min(capped[:, half_cols(a)], banks[a], a, 0)
        for a in range(SHEETS - 1):
            place(capped[:, half_cols(a)], a, 0)
        quantise(x_q[1, 1], 0, PASS, second_x.bitcast(BF16))
        take_min(second_x[:, half_cols(0)], banks[SHEETS - 1], SHEETS - 1, 0)
        place(second_x[:, half_cols(0)], SHEETS - 1, 0)
        lows = [capped[:, half_cols(0)], capped[:, half_cols(1)], larger[1]]
        banks = [last_product(a, 1) for a in range(SHEETS)]
        for a in range(SHEETS):
            take_min(lows[a], banks[a], a, 1)
        for a in range(SHEETS):
            place(lows[a], a, 1)
